import numpy as np
import ml_dtypes


def mxq(x, axis, fmt="e4m3"):
    dtype, down = {"e4m3": (ml_dtypes.float8_e4m3fn, 7), "e5m2": (ml_dtypes.float8_e5m2, 14)}[fmt]
    v = np.moveaxis(np.asarray(x, np.float32).astype(ml_dtypes.bfloat16).astype(np.float64), axis, -1)
    blocks = v.reshape(v.shape[:-1] + (-1, 32))
    amax = np.abs(blocks).max(-1, keepdims=True)
    byte = np.maximum(np.where(amax > 0, np.frexp(amax)[1] - 1 + 127, 0) - down, 1)
    scale = np.exp2(byte - 127.0)
    codes = (blocks / scale).astype(np.float32).astype(dtype).astype(np.float64)
    return np.moveaxis((codes * scale).reshape(v.shape), -1, axis)


WIDE = False


def mx_kscale(k):
    if not WIDE:
        return np.ones(k)
    levels = np.array([10, -10, 5, -5, 0])
    if k % 512:
        return np.exp2(np.random.permutation(np.resize(levels, k // 32))).repeat(32)
    a = np.empty((k // 512, 16))
    for p in range(k // 512):
        a[p, :8] = np.random.permutation(np.resize(levels, 8))
        for g in range(8):
            far = levels[np.abs(levels - a[p, g]) >= 10]
            a[p, g + 8] = far[np.random.randint(len(far))]
    return np.exp2(a.ravel()).repeat(32)


def f64(x):
    return np.asarray(x).astype(np.float64)


E2M1 = np.array([0.0, 0.5, 1.0, 1.5, 2.0, 3.0, 4.0, 6.0, -0.0, -0.5, -1.0, -1.5, -2.0, -3.0, -4.0, -6.0])


def pack_weight(w, fmt):
    k, n = w.shape
    w = f64(np.asarray(w, np.float32).astype(ml_dtypes.bfloat16)).reshape(k // 32, 32, n)
    amax = np.abs(w).max(1)
    if fmt == "e4m3":
        byte = np.frexp(amax)[1] - 1 + 127 - 7
    else:
        mant, ex = np.frexp(amax / 6.0)
        byte = np.where(mant > 0.5, ex, ex - 1) + 127
    byte = np.clip(np.where(amax > 0, byte, 1), 1, 254)
    scaled = (w * np.exp2(127.0 - byte)[:, None, :]).reshape(k, n).astype(np.float32)
    by_word = np.ascontiguousarray(scaled.reshape(k // 512, 128, 4, n).transpose(0, 1, 3, 2))
    if fmt == "e4m3":
        words = by_word.astype(ml_dtypes.float8_e4m3fn).view(np.uint8)
    else:
        c = by_word.astype(ml_dtypes.float4_e2m1fn).view(np.uint8) & 0xF
        words = (c[..., 0::2] | (c[..., 1::2] << 4)).reshape(k // 512, 128, 2 * n)
    return np.ascontiguousarray(words), np.ascontiguousarray(byte.astype(np.uint8).reshape(k // 512, 16, n))


def unpack_weight(words, scales, fmt):
    g, _, n = scales.shape
    words = np.ascontiguousarray(words).reshape(g, 128, n, -1)
    if fmt == "e4m3":
        vals = words.view(ml_dtypes.float8_e4m3fn).astype(np.float64)
    else:
        nib = np.empty((g, 128, n, 4), np.uint8)
        nib[..., 0::2] = words & 0xF
        nib[..., 1::2] = words >> 4
        vals = E2M1[nib]
    vals = vals * np.repeat(np.exp2(scales.astype(np.float64) - 127.0), 8, axis=1)[..., None]
    return vals.transpose(0, 1, 3, 2).reshape(g * 512, n)


O, K, M, T = 512, 2048, 512, 512


def setup_inputs():
    n = np.random.standard_normal
    s = mx_kscale(K)[:, None]
    x = n((K, T)); x[:O] *= 6.0
    w = n((K, M)) / np.sqrt(K) / s; w[:O] /= 2.0
    p_x4 = pack_weight(x[O:] * s[O:], "e2m1")
    p_w4 = pack_weight(w[O:], "e2m1")
    return {
        "x8": (x[:O] * s[:O]).astype(np.float32),
        "w8": (w[:O]).astype(np.float32),
        "x4_words": p_x4[0],
        "x4_scales": p_x4[1],
        "w4_words": p_w4[0],
        "w4_scales": p_w4[1],
    }


def reference(x8, w8, x4_words, x4_scales, w4_words, w4_scales):
    x8_ = mxq(f64(x8), 0, "e4m3")
    w8_ = mxq(f64(w8), 0, "e4m3")
    x4_ = unpack_weight(x4_words, x4_scales, "e2m1")
    w4_ = unpack_weight(w4_words, w4_scales, "e2m1")
    y = w8_.T @ x8_ + w4_.T @ x4_
    return y

@@ -1,0 +1,147 @@
+from contextlib import ExitStack
+
+import concourse.mybir as mybir
+
+O, K4, M, T = 512, 1536, 512, 512
+FLOPS = 2 * M * T * (O + K4)
+
+F32 = mybir.dt.float32
+BF16 = mybir.dt.bfloat16
+U32 = mybir.dt.uint32
+I32 = mybir.dt.int32
+U8 = mybir.dt.uint8
+FP8X4 = mybir.dt.float8_e4m3fn_x4
+FP4X4 = mybir.dt.float4_e2m1fn_x4
+
+P = 128
+PASSES4 = K4 // 512
+
+
+def tile_mix_atom_fm_none_kernel(tc, x8, w8, x4_words, x4_scales, w4_words, w4_scales, out):
+    nc = tc.nc
+    with ExitStack() as ctx:
+        keep = ctx.enter_context(tc.tile_pool(name="keep", bufs=1))
+        psum = ctx.enter_context(tc.psum_pool(name="psum", bufs=1))
+        ctx.enter_context(tc.manual_schedule())
+
+        x4w = keep.tile([P, PASSES4 * 2 * T], U8, align_bytes=64, name="x4w")
+        w4w = keep.tile([P, PASSES4 * 2 * M], U8, align_bytes=64, name="w4w")
+        x4s = keep.tile([P, PASSES4 * T], U8, align_bytes=64, name="x4s")
+        w4s = keep.tile([P, PASSES4 * M], U8, align_bytes=64, name="w4s")
+        x_raw = keep.tile([P, 4, T], F32, align_bytes=64, name="x_raw")
+        w_raw = [keep.tile([P, 4, 256], F32, align_bytes=64, name="w_raw%d" % h) for h in range(2)]
+
+        def memset0(tile):
+            nc.vector.memset(tile[:].bitcast(I32), 0)
+
+        warm_in = keep.tile([P, 1024], BF16, align_bytes=64, name="warm_in")
+        warm_codes = keep.tile([P, 256], U32, align_bytes=64, name="warm_codes")
+        warm_planes = keep.tile([P, 256], U8, align_bytes=64, name="warm_planes")
+        junk = psum.tile([P, 256], F32, name="junk")
+        memset0(x4s)
+        memset0(warm_in)
+        memset0(w4s)
+        nc.vector.quantize_mx(out=warm_codes[:].bitcast(FP8X4), scales=warm_planes[:], in_=warm_in[:])
+        for i in range(12):
+            nc.tensor.matmul_mx(
+                out=junk[:],
+                lhsT=warm_codes[:, 0:128].bitcast(FP8X4),
+                lhsT_scale=warm_planes[:, 0:128],
+                rhs=warm_codes[:].bitcast(FP8X4),
+                rhs_scale=warm_planes[:],
+                start=True,
+                stop=True,
+            )
+        w8_rows = w8.rearrange("(p j) n -> p j n", j=4)
+        x4s_rows = x4_scales.bitcast(I32).rearrange("a q n -> q a n")
+        w4s_rows = w4_scales.bitcast(I32).rearrange("a q n -> q a n")
+
+        def words(queue, tile, src):
+            queue.dma_start(out=tile[:].bitcast(I32).rearrange("p (a c) -> p a c", a=PASSES4), in_=src.bitcast(I32).rearrange("a p c -> p a c"))
+
+        def scale_rows(queue, plane, rows, q):
+            queue.dma_start(out=plane[32 * q : 32 * q + 4, :].bitcast(I32).rearrange("p (a n) -> p a n", a=PASSES4), in_=rows[4 * q : 4 * q + 4])
+
+        words(nc.sync, x4w, x4_words)
+        words(nc.gpsimd, w4w, w4_words)
+        scale_rows(nc.sync, x4s, x4s_rows, 0)
+        scale_rows(nc.sync, x4s, x4s_rows, 1)
+        scale_rows(nc.sync, x4s, x4s_rows, 2)
+        scale_rows(nc.sync, x4s, x4s_rows, 3)
+        scale_rows(nc.sync, w4s, w4s_rows, 0)
+        scale_rows(nc.sync, w4s, w4s_rows, 1)
+        scale_rows(nc.sync, w4s, w4s_rows, 2)
+        scale_rows(nc.sync, w4s, w4s_rows, 3)
+        nc.gpsimd.dma_start(out=x_raw[:], in_=x8.rearrange("(p j) t -> p j t", j=4))
+        nc.gpsimd.dma_start(out=w_raw[0][:], in_=w8_rows[:, :, 0:256])
+        nc.gpsimd.dma_start(out=w_raw[1][:], in_=w8_rows[:, :, 256:512])
+
+        warm = keep.tile([P, 8], F32, name="warm")
+        nc.vector.memset(warm[:], 0.0)
+        nc.scalar.copy(warm[:, 4:5], warm[:, 0:1])
+
+        acc = {}
+        for m in range(4):
+            for t0, n in ([(0, 512)] if m < 2 else [(0, 256), (256, 256)]):
+                acc[m, t0] = (psum.tile([P, n], F32, name="acc%d_%d" % (m, t0)), n)
+
+        for (m, t0), (bank, n) in acc.items():
+            for a in range(PASSES4):
+                nc.tensor.matmul_mx(
+                    out=bank[:],
+                    lhsT=w4w[:, 1024 * a + 256 * m : 1024 * a + 256 * m + 256].bitcast(FP4X4),
+                    lhsT_scale=w4s[:, 512 * a + 128 * m : 512 * a + 128 * m + 128],
+                    rhs=x4w[:, 1024 * a + 2 * t0 : 1024 * a + 2 * (t0 + n)].bitcast(FP4X4),
+                    rhs_scale=x4s[:, 512 * a + t0 : 512 * a + t0 + n],
+                    start=(a == 0),
+                    stop=False,
+                )
+
+        def interleave(copy, dst, c0, src, s0, n):
+            copy(
+                dst[:, 4 * c0 : 4 * (c0 + n)].rearrange("p (c i t) -> p c t i", i=4, t=4),
+                src[:, :, s0 : s0 + n].rearrange("p t (c i) -> p c t i", i=4),
+            )
+
+        x_codes = keep.tile([P, T], U32, align_bytes=64, name="x_codes")
+        x_planes = keep.tile([P, T], U8, align_bytes=64, name="x_planes")
+        xg = [keep.tile([P, 1024], BF16, align_bytes=64, name="xg%d" % h) for h in range(2)]
+        interleave(nc.vector.tensor_copy, xg[0], 0, x_raw, 0, 256)
+        interleave(nc.scalar.copy, xg[1], 64, x_raw, 320, 192)
+        interleave(nc.vector.tensor_copy, xg[1], 0, x_raw, 256, 64)
+        for h in range(2):
+            cols = slice(256 * h, 256 * h + 256)
+            nc.vector.quantize_mx(out=x_codes[:, cols].bitcast(FP8X4), scales=x_planes[:, cols], in_=xg[h][:])
+
+        w_codes = keep.tile([P, M], U32, align_bytes=64, name="w_codes")
+        w_planes = keep.tile([P, M], U8, align_bytes=64, name="w_planes")
+        res = [keep.tile([P, T], F32, name="res%d" % m) for m in range(4)]
+        for h in range(2):
+            wg = [keep.tile([P, 512], BF16, align_bytes=64, name="wg%d_%d" % (h, i)) for i in range(2)]
+            interleave(nc.vector.tensor_copy, wg[0], 0, w_raw[h], 0, 128)
+            interleave(nc.scalar.copy, wg[1], 32, w_raw[h], 160, 96)
+            interleave(nc.vector.tensor_copy, wg[1], 0, w_raw[h], 128, 32)
+            for i in range(2):
+                cols = slice(256 * h + 128 * i, 256 * h + 128 * i + 128)
+                nc.vector.quantize_mx(out=w_codes[:, cols].bitcast(FP8X4), scales=w_planes[:, cols], in_=wg[i][:])
+            for m in (2 * h, 2 * h + 1):
+                cols = slice(128 * m, 128 * m + 128)
+                for t0 in ((0,) if h == 0 else (0, 256)):
+                    bank, n = acc[m, t0]
+                    nc.tensor.matmul_mx(
+                        out=bank[:],
+                        lhsT=w_codes[:, cols].bitcast(FP8X4),
+                        lhsT_scale=w_planes[:, cols],
+                        rhs=x_codes[:, t0 : t0 + n].bitcast(FP8X4),
+                        rhs_scale=x_planes[:, t0 : t0 + n],
+                        start=False,
+                        stop=True,
+                    )
+        nc.scalar.copy(res[0][:], acc[0, 0][0][:])
+        nc.sync.dma_start(out=out[0:128, :], in_=res[0][:])
+        nc.vector.tensor_copy(res[1][:], acc[1, 0][0][:])
+        nc.sync.dma_start(out=out[128:256, :], in_=res[1][:])
+        for m in (2, 3):
+            nc.scalar.copy(res[m][:, 0:256], acc[m, 0][0][:])
+            nc.vector.tensor_copy(res[m][:, 256:512], acc[m, 256][0][:])
+            nc.sync.dma_start(out=out[128 * m : 128 * m + 128, :], in_=res[m][:])

@@ -31,27 +31,6 @@ def tile_mix_atom_fm_none_kernel(tc, x8, w8, x4_words, x4_scales, w4_words, w4_s
         x_raw = keep.tile([P, 4, T], F32, align_bytes=64, name="x_raw")
         w_raw = [keep.tile([P, 4, 256], F32, align_bytes=64, name="w_raw%d" % h) for h in range(2)]
 
-        def memset0(tile):
-            nc.vector.memset(tile[:].bitcast(I32), 0)
-
-        warm_in = keep.tile([P, 1024], BF16, align_bytes=64, name="warm_in")
-        warm_codes = keep.tile([P, 256], U32, align_bytes=64, name="warm_codes")
-        warm_planes = keep.tile([P, 256], U8, align_bytes=64, name="warm_planes")
-        junk = psum.tile([P, 256], F32, name="junk")
-        memset0(x4s)
-        memset0(warm_in)
-        memset0(w4s)
-        nc.vector.quantize_mx(out=warm_codes[:].bitcast(FP8X4), scales=warm_planes[:], in_=warm_in[:])
-        for i in range(12):
-            nc.tensor.matmul_mx(
-                out=junk[:],
-                lhsT=warm_codes[:, 0:128].bitcast(FP8X4),
-                lhsT_scale=warm_planes[:, 0:128],
-                rhs=warm_codes[:].bitcast(FP8X4),
-                rhs_scale=warm_planes[:],
-                start=True,
-                stop=True,
-            )
         w8_rows = w8.rearrange("(p j) n -> p j n", j=4)
         x4s_rows = x4_scales.bitcast(I32).rearrange("a q n -> q a n")
         w4s_rows = w4_scales.bitcast(I32).rearrange("a q n -> q a n")
@@ -62,8 +41,7 @@ def tile_mix_atom_fm_none_kernel(tc, x8, w8, x4_words, x4_scales, w4_words, w4_s
         def scale_rows(queue, plane, rows, q):
             queue.dma_start(out=plane[32 * q : 32 * q + 4, :].bitcast(I32).rearrange("p (a n) -> p a n", a=PASSES4), in_=rows[4 * q : 4 * q + 4])
 
-        words(nc.sync, x4w, x4_words)
-        words(nc.gpsimd, w4w, w4_words)
+        words(nc.gpsimd, x4w, x4_words)
         scale_rows(nc.sync, x4s, x4s_rows, 0)
         scale_rows(nc.sync, x4s, x4s_rows, 1)
         scale_rows(nc.sync, x4s, x4s_rows, 2)
@@ -72,30 +50,48 @@ def tile_mix_atom_fm_none_kernel(tc, x8, w8, x4_words, x4_scales, w4_words, w4_s
         scale_rows(nc.sync, w4s, w4s_rows, 1)
         scale_rows(nc.sync, w4s, w4s_rows, 2)
         scale_rows(nc.sync, w4s, w4s_rows, 3)
-        nc.gpsimd.dma_start(out=x_raw[:], in_=x8.rearrange("(p j) t -> p j t", j=4))
-        nc.gpsimd.dma_start(out=w_raw[0][:], in_=w8_rows[:, :, 0:256])
-        nc.gpsimd.dma_start(out=w_raw[1][:], in_=w8_rows[:, :, 256:512])
+        words(nc.sync, w4w, w4_words)
+        nc.sync.dma_start(out=x_raw[:], in_=x8.rearrange("(p j) t -> p j t", j=4))
+        nc.sync.dma_start(out=w_raw[0][:], in_=w8_rows[:, :, 0:256])
+        nc.sync.dma_start(out=w_raw[1][:], in_=w8_rows[:, :, 256:512])
 
+        warm_in = keep.tile([P, 1024], BF16, align_bytes=64, name="warm_in")
+        warm_codes = keep.tile([P, 256], U32, align_bytes=64, name="warm_codes")
+        warm_planes = keep.tile([P, 256], U8, align_bytes=64, name="warm_planes")
+        junk = psum.tile([P, 256], F32, name="junk")
+        nc.vector.memset(warm_in[:].bitcast(I32), 0)
         warm = keep.tile([P, 8], F32, name="warm")
-        nc.vector.memset(warm[:], 0.0)
-        nc.scalar.copy(warm[:, 4:5], warm[:, 0:1])
+        nc.scalar.copy(warm[:, 0:1], warm_in[:, 0:2].bitcast(F32))
+        nc.vector.quantize_mx(out=warm_codes[:].bitcast(FP8X4), scales=warm_planes[:], in_=warm_in[:])
+        for i in range(10):
+            nc.tensor.matmul_mx(
+                out=junk[:],
+                lhsT=warm_codes[:, 0:128].bitcast(FP8X4),
+                lhsT_scale=warm_planes[:, 0:128],
+                rhs=warm_codes[:].bitcast(FP8X4),
+                rhs_scale=warm_planes[:],
+                start=True,
+                stop=True,
+            )
 
         acc = {}
         for m in range(4):
             for t0, n in ([(0, 512)] if m < 2 else [(0, 256), (256, 256)]):
                 acc[m, t0] = (psum.tile([P, n], F32, name="acc%d_%d" % (m, t0)), n)
 
-        for (m, t0), (bank, n) in acc.items():
-            for a in range(PASSES4):
-                nc.tensor.matmul_mx(
-                    out=bank[:],
-                    lhsT=w4w[:, 1024 * a + 256 * m : 1024 * a + 256 * m + 256].bitcast(FP4X4),
-                    lhsT_scale=w4s[:, 512 * a + 128 * m : 512 * a + 128 * m + 128],
-                    rhs=x4w[:, 1024 * a + 2 * t0 : 1024 * a + 2 * (t0 + n)].bitcast(FP4X4),
-                    rhs_scale=x4s[:, 512 * a + t0 : 512 * a + t0 + n],
-                    start=(a == 0),
-                    stop=False,
-                )
+        def fp4_passes(m):
+            for t0 in ((0,) if m < 2 else (0, 256)):
+                bank, n = acc[m, t0]
+                for a in range(PASSES4):
+                    nc.tensor.matmul_mx(
+                        out=bank[:],
+                        lhsT=w4w[:, 1024 * a + 256 * m : 1024 * a + 256 * m + 256].bitcast(FP4X4),
+                        lhsT_scale=w4s[:, 512 * a + 128 * m : 512 * a + 128 * m + 128],
+                        rhs=x4w[:, 1024 * a + 2 * t0 : 1024 * a + 2 * (t0 + n)].bitcast(FP4X4),
+                        rhs_scale=x4s[:, 512 * a + t0 : 512 * a + t0 + n],
+                        start=(a == 0),
+                        stop=False,
+                    )
 
         def interleave(copy, dst, c0, src, s0, n):
             copy(
@@ -106,42 +102,57 @@ def tile_mix_atom_fm_none_kernel(tc, x8, w8, x4_words, x4_scales, w4_words, w4_s
         x_codes = keep.tile([P, T], U32, align_bytes=64, name="x_codes")
         x_planes = keep.tile([P, T], U8, align_bytes=64, name="x_planes")
         xg = [keep.tile([P, 1024], BF16, align_bytes=64, name="xg%d" % h) for h in range(2)]
-        interleave(nc.vector.tensor_copy, xg[0], 0, x_raw, 0, 256)
-        interleave(nc.scalar.copy, xg[1], 64, x_raw, 320, 192)
-        interleave(nc.vector.tensor_copy, xg[1], 0, x_raw, 256, 64)
-        for h in range(2):
+        w_codes = [keep.tile([P, 128], U32, align_bytes=64, name="w_codes%d" % m) for m in range(4)]
+        w_planes = [keep.tile([P, 128], U8, align_bytes=64, name="w_planes%d" % m) for m in range(4)]
+        wg = [keep.tile([P, 512], BF16, align_bytes=64, name="wg%d" % m) for m in range(4)]
+        res = [keep.tile([P, T], F32, name="res%d" % m) for m in range(4)]
+
+        def quant_x(h):
             cols = slice(256 * h, 256 * h + 256)
             nc.vector.quantize_mx(out=x_codes[:, cols].bitcast(FP8X4), scales=x_planes[:, cols], in_=xg[h][:])
 
-        w_codes = keep.tile([P, M], U32, align_bytes=64, name="w_codes")
-        w_planes = keep.tile([P, M], U8, align_bytes=64, name="w_planes")
-        res = [keep.tile([P, T], F32, name="res%d" % m) for m in range(4)]
-        for h in range(2):
-            wg = [keep.tile([P, 512], BF16, align_bytes=64, name="wg%d_%d" % (h, i)) for i in range(2)]
-            interleave(nc.vector.tensor_copy, wg[0], 0, w_raw[h], 0, 128)
-            interleave(nc.scalar.copy, wg[1], 32, w_raw[h], 160, 96)
-            interleave(nc.vector.tensor_copy, wg[1], 0, w_raw[h], 128, 32)
-            for i in range(2):
-                cols = slice(256 * h + 128 * i, 256 * h + 128 * i + 128)
-                nc.vector.quantize_mx(out=w_codes[:, cols].bitcast(FP8X4), scales=w_planes[:, cols], in_=wg[i][:])
-            for m in (2 * h, 2 * h + 1):
-                cols = slice(128 * m, 128 * m + 128)
-                for t0 in ((0,) if h == 0 else (0, 256)):
-                    bank, n = acc[m, t0]
-                    nc.tensor.matmul_mx(
-                        out=bank[:],
-                        lhsT=w_codes[:, cols].bitcast(FP8X4),
-                        lhsT_scale=w_planes[:, cols],
-                        rhs=x_codes[:, t0 : t0 + n].bitcast(FP8X4),
-                        rhs_scale=x_planes[:, t0 : t0 + n],
-                        start=False,
-                        stop=True,
-                    )
-        nc.scalar.copy(res[0][:], acc[0, 0][0][:])
-        nc.sync.dma_start(out=out[0:128, :], in_=res[0][:])
-        nc.vector.tensor_copy(res[1][:], acc[1, 0][0][:])
-        nc.sync.dma_start(out=out[128:256, :], in_=res[1][:])
+        def quant_w(m):
+            nc.vector.quantize_mx(out=w_codes[m][:].bitcast(FP8X4), scales=w_planes[m][:], in_=wg[m][:])
+
+        def fp8_pass(m):
+            for t0 in ((0,) if m < 2 else (0, 256)):
+                bank, n = acc[m, t0]
+                nc.tensor.matmul_mx(
+                    out=bank[:],
+                    lhsT=w_codes[m][:].bitcast(FP8X4),
+                    lhsT_scale=w_planes[m][:],
+                    rhs=x_codes[:, t0 : t0 + n].bitcast(FP8X4),
+                    rhs_scale=x_planes[:, t0 : t0 + n],
+                    start=False,
+                    stop=True,
+                )
+
+        def store(m):
+            nc.sync.dma_start(out=out[128 * m : 128 * m + 128, :], in_=res[m][:])
+
+        for m in range(4):
+            fp4_passes(m)
+        interleave(nc.vector.tensor_copy, xg[0], 0, x_raw, 0, 256)
+        interleave(nc.scalar.copy, xg[1], 64, x_raw, 320, 192)
+        interleave(nc.vector.tensor_copy, xg[1], 0, x_raw, 256, 64)
+        quant_x(0)
+        quant_x(1)
+        interleave(nc.vector.tensor_copy, wg[0], 0, w_raw[0], 0, 128)
+        interleave(nc.scalar.copy, wg[1], 32, w_raw[0], 160, 96)
+        interleave(nc.vector.tensor_copy, wg[1], 0, w_raw[0], 128, 32)
+        quant_w(0)
+        quant_w(1)
+        fp8_pass(0)
+        fp8_pass(1)
+        interleave(nc.vector.tensor_copy, wg[2], 0, w_raw[1], 0, 128)
+        interleave(nc.vector.tensor_copy, wg[3], 0, w_raw[1], 128, 128)
+        quant_w(2)
+        quant_w(3)
+        for m in (0, 1):
+            nc.scalar.copy(res[m][:], acc[m, 0][0][:])
+            store(m)
         for m in (2, 3):
+            fp8_pass(m)
             nc.scalar.copy(res[m][:, 0:256], acc[m, 0][0][:])
             nc.vector.tensor_copy(res[m][:, 256:512], acc[m, 256][0][:])
-            nc.sync.dma_start(out=out[128 * m : 128 * m + 128, :], in_=res[m][:])
+            store(m)

@@ -32,28 +32,28 @@ def tile_mix_atom_fm_none_kernel(tc, x8, w8, x4_words, x4_scales, w4_words, w4_s
         w_raw = [keep.tile([P, 4, 256], F32, align_bytes=64, name="w_raw%d" % h) for h in range(2)]
 
         w8_rows = w8.rearrange("(p j) n -> p j n", j=4)
-        x4s_rows = x4_scales.bitcast(I32).rearrange("a q n -> q a n")
-        w4s_rows = w4_scales.bitcast(I32).rearrange("a q n -> q a n")
+        x4s_rows = x4_scales.bitcast(I32).rearrange("a (q r) n -> r q a n", r=4)
+        w4s_rows = w4_scales.bitcast(I32).rearrange("a (q r) n -> r q a n", r=4)
 
         def words(queue, tile, src):
             queue.dma_start(out=tile[:].bitcast(I32).rearrange("p (a c) -> p a c", a=PASSES4), in_=src.bitcast(I32).rearrange("a p c -> p a c"))
 
-        def scale_rows(queue, plane, rows, q):
-            queue.dma_start(out=plane[32 * q : 32 * q + 4, :].bitcast(I32).rearrange("p (a n) -> p a n", a=PASSES4), in_=rows[4 * q : 4 * q + 4])
+        def scale_rows(queue, plane, rows, r):
+            queue.dma_start(out=plane[r:P:32, :].bitcast(I32).rearrange("p (a n) -> p a n", a=PASSES4), in_=rows[r])
 
-        words(nc.gpsimd, x4w, x4_words)
+        nc.gpsimd.dma_start(out=x_raw[:], in_=x8.rearrange("(p j) t -> p j t", j=4))
         scale_rows(nc.sync, x4s, x4s_rows, 0)
         scale_rows(nc.sync, x4s, x4s_rows, 1)
+        words(nc.sync, x4w, x4_words)
+        words(nc.sync, w4w, w4_words)
         scale_rows(nc.sync, x4s, x4s_rows, 2)
         scale_rows(nc.sync, x4s, x4s_rows, 3)
         scale_rows(nc.sync, w4s, w4s_rows, 0)
         scale_rows(nc.sync, w4s, w4s_rows, 1)
         scale_rows(nc.sync, w4s, w4s_rows, 2)
         scale_rows(nc.sync, w4s, w4s_rows, 3)
-        words(nc.sync, w4w, w4_words)
-        nc.sync.dma_start(out=x_raw[:], in_=x8.rearrange("(p j) t -> p j t", j=4))
-        nc.sync.dma_start(out=w_raw[0][:], in_=w8_rows[:, :, 0:256])
-        nc.sync.dma_start(out=w_raw[1][:], in_=w8_rows[:, :, 256:512])
+        nc.gpsimd.dma_start(out=w_raw[0][:], in_=w8_rows[:, :, 0:256])
+        nc.gpsimd.dma_start(out=w_raw[1][:], in_=w8_rows[:, :, 256:512])
 
         warm_in = keep.tile([P, 1024], BF16, align_bytes=64, name="warm_in")
         warm_codes = keep.tile([P, 256], U32, align_bytes=64, name="warm_codes")
@@ -63,7 +63,7 @@ def tile_mix_atom_fm_none_kernel(tc, x8, w8, x4_words, x4_scales, w4_words, w4_s
         warm = keep.tile([P, 8], F32, name="warm")
         nc.scalar.copy(warm[:, 0:1], warm_in[:, 0:2].bitcast(F32))
         nc.vector.quantize_mx(out=warm_codes[:].bitcast(FP8X4), scales=warm_planes[:], in_=warm_in[:])
-        for i in range(10):
+        for i in range(12):
             nc.tensor.matmul_mx(
                 out=junk[:],
                 lhsT=warm_codes[:, 0:128].bitcast(FP8X4),

@@ -41,19 +41,19 @@ def tile_mix_atom_fm_none_kernel(tc, x8, w8, x4_words, x4_scales, w4_words, w4_s
         def scale_rows(queue, plane, rows, r):
             queue.dma_start(out=plane[r:P:32, :].bitcast(I32).rearrange("p (a n) -> p a n", a=PASSES4), in_=rows[r])
 
-        nc.gpsimd.dma_start(out=x_raw[:], in_=x8.rearrange("(p j) t -> p j t", j=4))
+        words(nc.gpsimd, w4w, w4_words)
         scale_rows(nc.sync, x4s, x4s_rows, 0)
-        scale_rows(nc.sync, x4s, x4s_rows, 1)
         words(nc.sync, x4w, x4_words)
-        words(nc.sync, w4w, w4_words)
+        scale_rows(nc.sync, x4s, x4s_rows, 1)
         scale_rows(nc.sync, x4s, x4s_rows, 2)
         scale_rows(nc.sync, x4s, x4s_rows, 3)
         scale_rows(nc.sync, w4s, w4s_rows, 0)
         scale_rows(nc.sync, w4s, w4s_rows, 1)
         scale_rows(nc.sync, w4s, w4s_rows, 2)
         scale_rows(nc.sync, w4s, w4s_rows, 3)
-        nc.gpsimd.dma_start(out=w_raw[0][:], in_=w8_rows[:, :, 0:256])
-        nc.gpsimd.dma_start(out=w_raw[1][:], in_=w8_rows[:, :, 256:512])
+        nc.sync.dma_start(out=x_raw[:], in_=x8.rearrange("(p j) t -> p j t", j=4))
+        nc.sync.dma_start(out=w_raw[0][:], in_=w8_rows[:, :, 0:256])
+        nc.sync.dma_start(out=w_raw[1][:], in_=w8_rows[:, :, 256:512])
 
         warm_in = keep.tile([P, 1024], BF16, align_bytes=64, name="warm_in")
         warm_codes = keep.tile([P, 256], U32, align_bytes=64, name="warm_codes")

@@ -24,26 +24,26 @@ def tile_mix_atom_fm_none_kernel(tc, x8, w8, x4_words, x4_scales, w4_words, w4_s
         psum = ctx.enter_context(tc.psum_pool(name="psum", bufs=1))
         ctx.enter_context(tc.manual_schedule())
 
-        x4w = keep.tile([P, PASSES4 * 2 * T], U8, align_bytes=64, name="x4w")
-        w4w = keep.tile([P, PASSES4 * 2 * M], U8, align_bytes=64, name="w4w")
+        x4w = [keep.tile([P, n * 2 * T], U8, align_bytes=64, name="x4w%d" % n) for n in (2, 1)]
+        w4w = [keep.tile([P, n * 2 * M], U8, align_bytes=64, name="w4w%d" % n) for n in (2, 1)]
         x4s = keep.tile([P, PASSES4 * T], U8, align_bytes=64, name="x4s")
         w4s = keep.tile([P, PASSES4 * M], U8, align_bytes=64, name="w4s")
         x_raw = keep.tile([P, 4, T], F32, align_bytes=64, name="x_raw")
-        w_raw = [keep.tile([P, 4, 256], F32, align_bytes=64, name="w_raw%d" % h) for h in range(2)]
+        w_raw = [keep.tile([P, 4, n], F32, align_bytes=64, name="w_raw%d" % h) for h, n in enumerate((256, 128, 128))]
 
         w8_rows = w8.rearrange("(p j) n -> p j n", j=4)
         x4s_rows = x4_scales.bitcast(I32).rearrange("a (q r) n -> r q a n", r=4)
         w4s_rows = w4_scales.bitcast(I32).rearrange("a (q r) n -> r q a n", r=4)
 
-        def words(queue, tile, src):
-            queue.dma_start(out=tile[:].bitcast(I32).rearrange("p (a c) -> p a c", a=PASSES4), in_=src.bitcast(I32).rearrange("a p c -> p a c"))
+        def words(queue, tile, src, a0, a1):
+            queue.dma_start(out=tile[:].bitcast(I32).rearrange("p (a c) -> p a c", a=a1 - a0), in_=src.bitcast(I32)[a0:a1].rearrange("a p c -> p a c"))
 
         def scale_rows(queue, plane, rows, r):
             queue.dma_start(out=plane[r:P:32, :].bitcast(I32).rearrange("p (a n) -> p a n", a=PASSES4), in_=rows[r])
 
-        words(nc.gpsimd, w4w, w4_words)
+        words(nc.gpsimd, w4w[0], w4_words, 0, 2)
         scale_rows(nc.sync, x4s, x4s_rows, 0)
-        words(nc.sync, x4w, x4_words)
+        words(nc.sync, x4w[0], x4_words, 0, 2)
         scale_rows(nc.sync, x4s, x4s_rows, 1)
         scale_rows(nc.sync, x4s, x4s_rows, 2)
         scale_rows(nc.sync, x4s, x4s_rows, 3)
@@ -53,7 +53,10 @@ def tile_mix_atom_fm_none_kernel(tc, x8, w8, x4_words, x4_scales, w4_words, w4_s
         scale_rows(nc.sync, w4s, w4s_rows, 3)
         nc.sync.dma_start(out=x_raw[:], in_=x8.rearrange("(p j) t -> p j t", j=4))
         nc.sync.dma_start(out=w_raw[0][:], in_=w8_rows[:, :, 0:256])
-        nc.sync.dma_start(out=w_raw[1][:], in_=w8_rows[:, :, 256:512])
+        words(nc.sync, x4w[1], x4_words, 2, 3)
+        words(nc.sync, w4w[1], w4_words, 2, 3)
+        nc.sync.dma_start(out=w_raw[1][:], in_=w8_rows[:, :, 256:384])
+        nc.sync.dma_start(out=w_raw[2][:], in_=w8_rows[:, :, 384:512])
 
         warm_in = keep.tile([P, 1024], BF16, align_bytes=64, name="warm_in")
         warm_codes = keep.tile([P, 256], U32, align_bytes=64, name="warm_codes")
@@ -79,18 +82,19 @@ def tile_mix_atom_fm_none_kernel(tc, x8, w8, x4_words, x4_scales, w4_words, w4_s
             for t0, n in ([(0, 512)] if m < 2 else [(0, 256), (256, 256)]):
                 acc[m, t0] = (psum.tile([P, n], F32, name="acc%d_%d" % (m, t0)), n)
 
-        def fp4_passes(m):
+        def fp4_passes(m, passes, stop=False):
             for t0 in ((0,) if m < 2 else (0, 256)):
                 bank, n = acc[m, t0]
-                for a in range(PASSES4):
+                for a in passes:
+                    c0 = 1024 * (a % 2)
                     nc.tensor.matmul_mx(
                         out=bank[:],
-                        lhsT=w4w[:, 1024 * a + 256 * m : 1024 * a + 256 * m + 256].bitcast(FP4X4),
+                        lhsT=w4w[a // 2][:, c0 + 256 * m : c0 + 256 * m + 256].bitcast(FP4X4),
                         lhsT_scale=w4s[:, 512 * a + 128 * m : 512 * a + 128 * m + 128],
-                        rhs=x4w[:, 1024 * a + 2 * t0 : 1024 * a + 2 * (t0 + n)].bitcast(FP4X4),
+                        rhs=x4w[a // 2][:, c0 + 2 * t0 : c0 + 2 * (t0 + n)].bitcast(FP4X4),
                         rhs_scale=x4s[:, 512 * a + t0 : 512 * a + t0 + n],
                         start=(a == 0),
-                        stop=False,
+                        stop=stop,
                     )
 
         def interleave(copy, dst, c0, src, s0, n):
@@ -114,7 +118,7 @@ def tile_mix_atom_fm_none_kernel(tc, x8, w8, x4_words, x4_scales, w4_words, w4_s
         def quant_w(m):
             nc.vector.quantize_mx(out=w_codes[m][:].bitcast(FP8X4), scales=w_planes[m][:], in_=wg[m][:])
 
-        def fp8_pass(m):
+        def fp8_pass(m, stop=True):
             for t0 in ((0,) if m < 2 else (0, 256)):
                 bank, n = acc[m, t0]
                 nc.tensor.matmul_mx(
@@ -124,6 +128,18 @@ def tile_mix_atom_fm_none_kernel(tc, x8, w8, x4_words, x4_scales, w4_words, w4_s
                     rhs=x_codes[:, t0 : t0 + n].bitcast(FP8X4),
                     rhs_scale=x_planes[:, t0 : t0 + n],
                     start=False,
+                    stop=stop,
+                )
+
+        def keep_warm(count):
+            for i in range(count):
+                nc.tensor.matmul_mx(
+                    out=junk[:],
+                    lhsT=warm_codes[:, 0:128].bitcast(FP8X4),
+                    lhsT_scale=warm_planes[:, 0:128],
+                    rhs=x_codes[:, 0:256].bitcast(FP8X4),
+                    rhs_scale=x_planes[:, 0:256],
+                    start=True,
                     stop=True,
                 )
 
@@ -131,23 +147,26 @@ def tile_mix_atom_fm_none_kernel(tc, x8, w8, x4_words, x4_scales, w4_words, w4_s
             nc.sync.dma_start(out=out[128 * m : 128 * m + 128, :], in_=res[m][:])
 
         for m in range(4):
-            fp4_passes(m)
+            fp4_passes(m, (0, 1))
         interleave(nc.vector.tensor_copy, xg[0], 0, x_raw, 0, 256)
         interleave(nc.scalar.copy, xg[1], 64, x_raw, 320, 192)
         interleave(nc.vector.tensor_copy, xg[1], 0, x_raw, 256, 64)
         quant_x(0)
+        keep_warm(4)
         quant_x(1)
         interleave(nc.vector.tensor_copy, wg[0], 0, w_raw[0], 0, 128)
         interleave(nc.scalar.copy, wg[1], 32, w_raw[0], 160, 96)
         interleave(nc.vector.tensor_copy, wg[1], 0, w_raw[0], 128, 32)
         quant_w(0)
         quant_w(1)
-        fp8_pass(0)
-        fp8_pass(1)
-        interleave(nc.vector.tensor_copy, wg[2], 0, w_raw[1], 0, 128)
-        interleave(nc.vector.tensor_copy, wg[3], 0, w_raw[1], 128, 128)
-        quant_w(2)
-        quant_w(3)
+        for m in (0, 1):
+            fp8_pass(m, stop=False)
+            fp4_passes(m, (2,), stop=True)
+        for m in (2, 3):
+            fp4_passes(m, (2,))
+        for m in (2, 3):
+            interleave(nc.vector.tensor_copy, wg[m], 0, w_raw[m - 1], 0, 128)
+            quant_w(m)
         for m in (0, 1):
             nc.scalar.copy(res[m][:], acc[m, 0][0][:])
             store(m)

@@ -43,15 +43,15 @@ def tile_mix_atom_fm_none_kernel(tc, x8, w8, x4_words, x4_scales, w4_words, w4_s
 
         words(nc.gpsimd, w4w[0], w4_words, 0, 2)
         scale_rows(nc.sync, x4s, x4s_rows, 0)
-        words(nc.sync, x4w[0], x4_words, 0, 2)
         scale_rows(nc.sync, x4s, x4s_rows, 1)
+        words(nc.sync, x4w[0], x4_words, 0, 2)
         scale_rows(nc.sync, x4s, x4s_rows, 2)
         scale_rows(nc.sync, x4s, x4s_rows, 3)
         scale_rows(nc.sync, w4s, w4s_rows, 0)
         scale_rows(nc.sync, w4s, w4s_rows, 1)
-        scale_rows(nc.sync, w4s, w4s_rows, 2)
-        scale_rows(nc.sync, w4s, w4s_rows, 3)
         nc.sync.dma_start(out=x_raw[:], in_=x8.rearrange("(p j) t -> p j t", j=4))
+        scale_rows(nc.scalar, w4s, w4s_rows, 2)
+        scale_rows(nc.scalar, w4s, w4s_rows, 3)
         nc.sync.dma_start(out=w_raw[0][:], in_=w8_rows[:, :, 0:256])
         words(nc.sync, x4w[1], x4_words, 2, 3)
         words(nc.sync, w4w[1], w4_words, 2, 3)
@@ -66,7 +66,7 @@ def tile_mix_atom_fm_none_kernel(tc, x8, w8, x4_words, x4_scales, w4_words, w4_s
         warm = keep.tile([P, 8], F32, name="warm")
         nc.scalar.copy(warm[:, 0:1], warm_in[:, 0:2].bitcast(F32))
         nc.vector.quantize_mx(out=warm_codes[:].bitcast(FP8X4), scales=warm_planes[:], in_=warm_in[:])
-        for i in range(12):
+        for i in range(24):
             nc.tensor.matmul_mx(
                 out=junk[:],
                 lhsT=warm_codes[:, 0:128].bitcast(FP8X4),
@@ -131,18 +131,6 @@ def tile_mix_atom_fm_none_kernel(tc, x8, w8, x4_words, x4_scales, w4_words, w4_s
                     stop=stop,
                 )
 
-        def keep_warm(count):
-            for i in range(count):
-                nc.tensor.matmul_mx(
-                    out=junk[:],
-                    lhsT=warm_codes[:, 0:128].bitcast(FP8X4),
-                    lhsT_scale=warm_planes[:, 0:128],
-                    rhs=x_codes[:, 0:256].bitcast(FP8X4),
-                    rhs_scale=x_planes[:, 0:256],
-                    start=True,
-                    stop=True,
-                )
-
         def store(m):
             nc.sync.dma_start(out=out[128 * m : 128 * m + 128, :], in_=res[m][:])
 
@@ -152,7 +140,6 @@ def tile_mix_atom_fm_none_kernel(tc, x8, w8, x4_words, x4_scales, w4_words, w4_s
         interleave(nc.scalar.copy, xg[1], 64, x_raw, 320, 192)
         interleave(nc.vector.tensor_copy, xg[1], 0, x_raw, 256, 64)
         quant_x(0)
-        keep_warm(4)
         quant_x(1)
         interleave(nc.vector.tensor_copy, wg[0], 0, w_raw[0], 0, 128)
         interleave(nc.scalar.copy, wg[1], 32, w_raw[0], 160, 96)

@@ -49,9 +49,10 @@ def tile_mix_atom_fm_none_kernel(tc, x8, w8, x4_words, x4_scales, w4_words, w4_s
         scale_rows(nc.sync, x4s, x4s_rows, 3)
         scale_rows(nc.sync, w4s, w4s_rows, 0)
         scale_rows(nc.sync, w4s, w4s_rows, 1)
-        nc.sync.dma_start(out=x_raw[:], in_=x8.rearrange("(p j) t -> p j t", j=4))
-        scale_rows(nc.scalar, w4s, w4s_rows, 2)
-        scale_rows(nc.scalar, w4s, w4s_rows, 3)
+        nc.sync.dma_start(out=x_raw[:, 0:2, :], in_=x8.rearrange("(p j) t -> p j t", j=4)[:, 0:2, :])
+        scale_rows(nc.sync, w4s, w4s_rows, 2)
+        scale_rows(nc.sync, w4s, w4s_rows, 3)
+        nc.sync.dma_start(out=x_raw[:, 2:4, :], in_=x8.rearrange("(p j) t -> p j t", j=4)[:, 2:4, :])
         nc.sync.dma_start(out=w_raw[0][:], in_=w8_rows[:, :, 0:256])
         words(nc.sync, x4w[1], x4_words, 2, 3)
         words(nc.sync, w4w[1], w4_words, 2, 3)
@@ -66,7 +67,7 @@ def tile_mix_atom_fm_none_kernel(tc, x8, w8, x4_words, x4_scales, w4_words, w4_s
         warm = keep.tile([P, 8], F32, name="warm")
         nc.scalar.copy(warm[:, 0:1], warm_in[:, 0:2].bitcast(F32))
         nc.vector.quantize_mx(out=warm_codes[:].bitcast(FP8X4), scales=warm_planes[:], in_=warm_in[:])
-        for i in range(24):
+        for i in range(16):
             nc.tensor.matmul_mx(
                 out=junk[:],
                 lhsT=warm_codes[:, 0:128].bitcast(FP8X4),
@@ -150,15 +151,16 @@ def tile_mix_atom_fm_none_kernel(tc, x8, w8, x4_words, x4_scales, w4_words, w4_s
             fp8_pass(m, stop=False)
             fp4_passes(m, (2,), stop=True)
         for m in (2, 3):
-            fp4_passes(m, (2,))
-        for m in (2, 3):
             interleave(nc.vector.tensor_copy, wg[m], 0, w_raw[m - 1], 0, 128)
             quant_w(m)
+            fp4_passes(m, (2,))
+            fp8_pass(m)
         for m in (0, 1):
             nc.scalar.copy(res[m][:], acc[m, 0][0][:])
             store(m)
-        for m in (2, 3):
-            fp8_pass(m)
-            nc.scalar.copy(res[m][:, 0:256], acc[m, 0][0][:])
-            nc.vector.tensor_copy(res[m][:, 256:512], acc[m, 256][0][:])
-            store(m)
+        for t0 in (0, 256):
+            nc.scalar.copy(res[2][:, t0 : t0 + 256], acc[2, t0][0][:])
+        store(2)
+        nc.scalar.copy(res[3][:, 0:256], acc[3, 0][0][:])
+        nc.vector.tensor_copy(res[3][:, 256:512], acc[3, 256][0][:])
+        store(3)

@@ -15,6 +15,7 @@ FP4X4 = mybir.dt.float4_e2m1fn_x4
 
 P = 128
 PASSES4 = K4 // 512
+H = T // 2
 
 
 def tile_mix_atom_fm_none_kernel(tc, x8, w8, x4_words, x4_scales, w4_words, w4_scales, out):
@@ -25,12 +26,14 @@ def tile_mix_atom_fm_none_kernel(tc, x8, w8, x4_words, x4_scales, w4_words, w4_s
         ctx.enter_context(tc.manual_schedule())
 
         x4w = [keep.tile([P, n * 2 * T], U8, align_bytes=64, name="x4w%d" % n) for n in (2, 1)]
-        w4w = [keep.tile([P, n * 2 * M], U8, align_bytes=64, name="w4w%d" % n) for n in (2, 1)]
+        w4w = keep.tile([P, 2 * 2 * M], U8, align_bytes=64, name="w4w")
+        w4w_last = [keep.tile([P, M], U8, align_bytes=64, name="w4w_last%d" % h) for h in range(2)]
         x4s = keep.tile([P, PASSES4 * T], U8, align_bytes=64, name="x4s")
         w4s = keep.tile([P, PASSES4 * M], U8, align_bytes=64, name="w4s")
-        x_raw = keep.tile([P, 4, T], F32, align_bytes=64, name="x_raw")
+        x_raw = [keep.tile([P, 4, H], F32, align_bytes=64, name="x_raw%d" % h) for h in range(2)]
         w_raw = [keep.tile([P, 4, n], F32, align_bytes=64, name="w_raw%d" % h) for h, n in enumerate((256, 128, 128))]
 
+        x8_rows = x8.rearrange("(p j) t -> p j t", j=4)
         w8_rows = w8.rearrange("(p j) n -> p j n", j=4)
         x4s_rows = x4_scales.bitcast(I32).rearrange("a (q r) n -> r q a n", r=4)
         w4s_rows = w4_scales.bitcast(I32).rearrange("a (q r) n -> r q a n", r=4)
@@ -41,23 +44,24 @@ def tile_mix_atom_fm_none_kernel(tc, x8, w8, x4_words, x4_scales, w4_words, w4_s
         def scale_rows(queue, plane, rows, r):
             queue.dma_start(out=plane[r:P:32, :].bitcast(I32).rearrange("p (a n) -> p a n", a=PASSES4), in_=rows[r])
 
-        words(nc.gpsimd, w4w[0], w4_words, 0, 2)
-        scale_rows(nc.sync, x4s, x4s_rows, 0)
+        words(nc.gpsimd, w4w, w4_words, 0, 2)
+        scale_rows(nc.scalar, x4s, x4s_rows, 0)
         scale_rows(nc.sync, x4s, x4s_rows, 1)
+        scale_rows(nc.scalar, x4s, x4s_rows, 2)
         words(nc.sync, x4w[0], x4_words, 0, 2)
-        scale_rows(nc.sync, x4s, x4s_rows, 2)
         scale_rows(nc.sync, x4s, x4s_rows, 3)
         scale_rows(nc.sync, w4s, w4s_rows, 0)
         scale_rows(nc.sync, w4s, w4s_rows, 1)
-        nc.sync.dma_start(out=x_raw[:, 0:2, :], in_=x8.rearrange("(p j) t -> p j t", j=4)[:, 0:2, :])
+        nc.sync.dma_start(out=x_raw[0][:], in_=x8_rows[:, :, 0:H])
         scale_rows(nc.sync, w4s, w4s_rows, 2)
         scale_rows(nc.sync, w4s, w4s_rows, 3)
-        nc.sync.dma_start(out=x_raw[:, 2:4, :], in_=x8.rearrange("(p j) t -> p j t", j=4)[:, 2:4, :])
+        nc.sync.dma_start(out=x_raw[1][:], in_=x8_rows[:, :, H:T])
         nc.sync.dma_start(out=w_raw[0][:], in_=w8_rows[:, :, 0:256])
         words(nc.sync, x4w[1], x4_words, 2, 3)
-        words(nc.sync, w4w[1], w4_words, 2, 3)
+        nc.sync.dma_start(out=w4w_last[0][:].bitcast(I32), in_=w4_words.bitcast(I32)[2, :, 0:128])
         nc.sync.dma_start(out=w_raw[1][:], in_=w8_rows[:, :, 256:384])
         nc.sync.dma_start(out=w_raw[2][:], in_=w8_rows[:, :, 384:512])
+        nc.sync.dma_start(out=w4w_last[1][:].bitcast(I32), in_=w4_words.bitcast(I32)[2, :, 128:256])
 
         warm_in = keep.tile([P, 1024], BF16, align_bytes=64, name="warm_in")
         warm_codes = keep.tile([P, 256], U32, align_bytes=64, name="warm_codes")
@@ -80,22 +84,26 @@ def tile_mix_atom_fm_none_kernel(tc, x8, w8, x4_words, x4_scales, w4_words, w4_s
 
         acc = {}
         for m in range(4):
-            for t0, n in ([(0, 512)] if m < 2 else [(0, 256), (256, 256)]):
+            for t0, n in ([(0, T)] if m < 2 else [(0, H), (H, H)]):
                 acc[m, t0] = (psum.tile([P, n], F32, name="acc%d_%d" % (m, t0)), n)
 
-        def fp4_passes(m, passes, stop=False):
-            for t0 in ((0,) if m < 2 else (0, 256)):
+        def fp4_passes(m, passes):
+            for t0 in ((0,) if m < 2 else (0, H)):
                 bank, n = acc[m, t0]
                 for a in passes:
                     c0 = 1024 * (a % 2)
+                    if a < 2:
+                        w_words = w4w[:, c0 + 256 * m : c0 + 256 * m + 256]
+                    else:
+                        w_words = w4w_last[m // 2][:, 256 * (m % 2) : 256 * (m % 2) + 256]
                     nc.tensor.matmul_mx(
                         out=bank[:],
-                        lhsT=w4w[a // 2][:, c0 + 256 * m : c0 + 256 * m + 256].bitcast(FP4X4),
+                        lhsT=w_words.bitcast(FP4X4),
                         lhsT_scale=w4s[:, 512 * a + 128 * m : 512 * a + 128 * m + 128],
                         rhs=x4w[a // 2][:, c0 + 2 * t0 : c0 + 2 * (t0 + n)].bitcast(FP4X4),
                         rhs_scale=x4s[:, 512 * a + t0 : 512 * a + t0 + n],
                         start=(a == 0),
-                        stop=stop,
+                        stop=False,
                     )
 
         def interleave(copy, dst, c0, src, s0, n):
@@ -106,21 +114,24 @@ def tile_mix_atom_fm_none_kernel(tc, x8, w8, x4_words, x4_scales, w4_words, w4_s
 
         x_codes = keep.tile([P, T], U32, align_bytes=64, name="x_codes")
         x_planes = keep.tile([P, T], U8, align_bytes=64, name="x_planes")
-        xg = [keep.tile([P, 1024], BF16, align_bytes=64, name="xg%d" % h) for h in range(2)]
+        xg = [keep.tile([P, 512], BF16, align_bytes=64, name="xg%d" % h) for h in range(4)]
         w_codes = [keep.tile([P, 128], U32, align_bytes=64, name="w_codes%d" % m) for m in range(4)]
         w_planes = [keep.tile([P, 128], U8, align_bytes=64, name="w_planes%d" % m) for m in range(4)]
         wg = [keep.tile([P, 512], BF16, align_bytes=64, name="wg%d" % m) for m in range(4)]
         res = [keep.tile([P, T], F32, name="res%d" % m) for m in range(4)]
 
-        def quant_x(h):
-            cols = slice(256 * h, 256 * h + 256)
-            nc.vector.quantize_mx(out=x_codes[:, cols].bitcast(FP8X4), scales=x_planes[:, cols], in_=xg[h][:])
+        def cast_x(q):
+            interleave(nc.vector.tensor_copy, xg[q], 0, x_raw[q // 2], 128 * (q % 2), 128)
+
+        def quant_x(q):
+            cols = slice(128 * q, 128 * q + 128)
+            nc.vector.quantize_mx(out=x_codes[:, cols].bitcast(FP8X4), scales=x_planes[:, cols], in_=xg[q][:])
 
         def quant_w(m):
             nc.vector.quantize_mx(out=w_codes[m][:].bitcast(FP8X4), scales=w_planes[m][:], in_=wg[m][:])
 
-        def fp8_pass(m, stop=True):
-            for t0 in ((0,) if m < 2 else (0, 256)):
+        def fp8_pass(m):
+            for t0 in ((0,) if m < 2 else (0, H)):
                 bank, n = acc[m, t0]
                 nc.tensor.matmul_mx(
                     out=bank[:],
@@ -129,7 +140,7 @@ def tile_mix_atom_fm_none_kernel(tc, x8, w8, x4_words, x4_scales, w4_words, w4_s
                     rhs=x_codes[:, t0 : t0 + n].bitcast(FP8X4),
                     rhs_scale=x_planes[:, t0 : t0 + n],
                     start=False,
-                    stop=stop,
+                    stop=True,
                 )
 
         def store(m):
@@ -137,30 +148,26 @@ def tile_mix_atom_fm_none_kernel(tc, x8, w8, x4_words, x4_scales, w4_words, w4_s
 
         for m in range(4):
             fp4_passes(m, (0, 1))
-        interleave(nc.vector.tensor_copy, xg[0], 0, x_raw, 0, 256)
-        interleave(nc.scalar.copy, xg[1], 64, x_raw, 320, 192)
-        interleave(nc.vector.tensor_copy, xg[1], 0, x_raw, 256, 64)
-        quant_x(0)
-        quant_x(1)
+        for h in range(2):
+            cast_x(2 * h)
+            cast_x(2 * h + 1)
+            quant_x(2 * h)
+            quant_x(2 * h + 1)
         interleave(nc.vector.tensor_copy, wg[0], 0, w_raw[0], 0, 128)
         interleave(nc.scalar.copy, wg[1], 32, w_raw[0], 160, 96)
         interleave(nc.vector.tensor_copy, wg[1], 0, w_raw[0], 128, 32)
         quant_w(0)
         quant_w(1)
-        for m in (0, 1):
-            fp8_pass(m, stop=False)
-            fp4_passes(m, (2,), stop=True)
         for m in (2, 3):
             interleave(nc.vector.tensor_copy, wg[m], 0, w_raw[m - 1], 0, 128)
             quant_w(m)
+        for m in range(4):
             fp4_passes(m, (2,))
             fp8_pass(m)
         for m in (0, 1):
             nc.scalar.copy(res[m][:], acc[m, 0][0][:])
             store(m)
-        for t0 in (0, 256):
-            nc.scalar.copy(res[2][:, t0 : t0 + 256], acc[2, t0][0][:])
-        store(2)
-        nc.scalar.copy(res[3][:, 0:256], acc[3, 0][0][:])
-        nc.vector.tensor_copy(res[3][:, 256:512], acc[3, 256][0][:])
-        store(3)
+        for m in (2, 3):
+            nc.scalar.copy(res[m][:, 0:H], acc[m, 0][0][:])
+            nc.vector.tensor_copy(res[m][:, H:T], acc[m, H][0][:])
+            store(m)

@@ -55,25 +55,29 @@ def tile_mix_atom_fm_none_kernel(tc, x8, w8, x4_words, x4_scales, w4_words, w4_s
         nc.sync.dma_start(out=x_raw[0][:], in_=x8_rows[:, :, 0:H])
         scale_rows(nc.sync, w4s, w4s_rows, 2)
         scale_rows(nc.sync, w4s, w4s_rows, 3)
-        nc.sync.dma_start(out=x_raw[1][:], in_=x8_rows[:, :, H:T])
         nc.sync.dma_start(out=w_raw[0][:], in_=w8_rows[:, :, 0:256])
+        nc.sync.dma_start(out=x_raw[1][:], in_=x8_rows[:, :, H:T])
         words(nc.sync, x4w[1], x4_words, 2, 3)
         nc.sync.dma_start(out=w4w_last[0][:].bitcast(I32), in_=w4_words.bitcast(I32)[2, :, 0:128])
         nc.sync.dma_start(out=w_raw[1][:], in_=w8_rows[:, :, 256:384])
         nc.sync.dma_start(out=w_raw[2][:], in_=w8_rows[:, :, 384:512])
         nc.sync.dma_start(out=w4w_last[1][:].bitcast(I32), in_=w4_words.bitcast(I32)[2, :, 128:256])
 
+        acc = {}
+        for m in range(4):
+            for h in range(2):
+                acc[m, h] = psum.tile([P, H], F32, name="acc%d_%d" % (m, h))
+
         warm_in = keep.tile([P, 1024], BF16, align_bytes=64, name="warm_in")
         warm_codes = keep.tile([P, 256], U32, align_bytes=64, name="warm_codes")
         warm_planes = keep.tile([P, 256], U8, align_bytes=64, name="warm_planes")
-        junk = psum.tile([P, 256], F32, name="junk")
         nc.vector.memset(warm_in[:].bitcast(I32), 0)
         warm = keep.tile([P, 8], F32, name="warm")
         nc.scalar.copy(warm[:, 0:1], warm_in[:, 0:2].bitcast(F32))
         nc.vector.quantize_mx(out=warm_codes[:].bitcast(FP8X4), scales=warm_planes[:], in_=warm_in[:])
         for i in range(16):
             nc.tensor.matmul_mx(
-                out=junk[:],
+                out=acc[3, 1][:],
                 lhsT=warm_codes[:, 0:128].bitcast(FP8X4),
                 lhsT_scale=warm_planes[:, 0:128],
                 rhs=warm_codes[:].bitcast(FP8X4),
@@ -82,29 +86,21 @@ def tile_mix_atom_fm_none_kernel(tc, x8, w8, x4_words, x4_scales, w4_words, w4_s
                 stop=True,
             )
 
-        acc = {}
-        for m in range(4):
-            for t0, n in ([(0, T)] if m < 2 else [(0, H), (H, H)]):
-                acc[m, t0] = (psum.tile([P, n], F32, name="acc%d_%d" % (m, t0)), n)
-
-        def fp4_passes(m, passes):
-            for t0 in ((0,) if m < 2 else (0, H)):
-                bank, n = acc[m, t0]
-                for a in passes:
-                    c0 = 1024 * (a % 2)
-                    if a < 2:
-                        w_words = w4w[:, c0 + 256 * m : c0 + 256 * m + 256]
-                    else:
-                        w_words = w4w_last[m // 2][:, 256 * (m % 2) : 256 * (m % 2) + 256]
-                    nc.tensor.matmul_mx(
-                        out=bank[:],
-                        lhsT=w_words.bitcast(FP4X4),
-                        lhsT_scale=w4s[:, 512 * a + 128 * m : 512 * a + 128 * m + 128],
-                        rhs=x4w[a // 2][:, c0 + 2 * t0 : c0 + 2 * (t0 + n)].bitcast(FP4X4),
-                        rhs_scale=x4s[:, 512 * a + t0 : 512 * a + t0 + n],
-                        start=(a == 0),
-                        stop=False,
-                    )
+        def fp4_pass(m, h, a, stop=False):
+            c0 = 1024 * (a % 2)
+            if a < 2:
+                w_words = w4w[:, c0 + 256 * m : c0 + 256 * m + 256]
+            else:
+                w_words = w4w_last[m // 2][:, 256 * (m % 2) : 256 * (m % 2) + 256]
+            nc.tensor.matmul_mx(
+                out=acc[m, h][:],
+                lhsT=w_words.bitcast(FP4X4),
+                lhsT_scale=w4s[:, 512 * a + 128 * m : 512 * a + 128 * m + 128],
+                rhs=x4w[a // 2][:, c0 + 2 * H * h : c0 + 2 * H * (h + 1)].bitcast(FP4X4),
+                rhs_scale=x4s[:, 512 * a + H * h : 512 * a + H * (h + 1)],
+                start=(a == 0),
+                stop=stop,
+            )
 
         def interleave(copy, dst, c0, src, s0, n):
             copy(
@@ -112,62 +108,71 @@ def tile_mix_atom_fm_none_kernel(tc, x8, w8, x4_words, x4_scales, w4_words, w4_s
                 src[:, :, s0 : s0 + n].rearrange("p t (c i) -> p c t i", i=4),
             )
 
-        x_codes = keep.tile([P, T], U32, align_bytes=64, name="x_codes")
-        x_planes = keep.tile([P, T], U8, align_bytes=64, name="x_planes")
+        x_codes = [keep.tile([P, H], U32, align_bytes=64, name="x_codes%d" % h) for h in range(2)]
+        x_planes = [keep.tile([P, H], U8, align_bytes=64, name="x_planes%d" % h) for h in range(2)]
         xg = [keep.tile([P, 512], BF16, align_bytes=64, name="xg%d" % h) for h in range(4)]
         w_codes = [keep.tile([P, 128], U32, align_bytes=64, name="w_codes%d" % m) for m in range(4)]
         w_planes = [keep.tile([P, 128], U8, align_bytes=64, name="w_planes%d" % m) for m in range(4)]
         wg = [keep.tile([P, 512], BF16, align_bytes=64, name="wg%d" % m) for m in range(4)]
-        res = [keep.tile([P, T], F32, name="res%d" % m) for m in range(4)]
-
-        def cast_x(q):
-            interleave(nc.vector.tensor_copy, xg[q], 0, x_raw[q // 2], 128 * (q % 2), 128)
+        res_top = [keep.tile([P, 2, H], F32, name="res_top%d" % h) for h in range(2)]
+        res = {m: keep.tile([P, T], F32, name="res%d" % m) for m in (2, 3)}
 
         def quant_x(q):
-            cols = slice(128 * q, 128 * q + 128)
-            nc.vector.quantize_mx(out=x_codes[:, cols].bitcast(FP8X4), scales=x_planes[:, cols], in_=xg[q][:])
+            cols = slice(128 * (q % 2), 128 * (q % 2) + 128)
+            nc.vector.quantize_mx(out=x_codes[q // 2][:, cols].bitcast(FP8X4), scales=x_planes[q // 2][:, cols], in_=xg[q][:])
 
         def quant_w(m):
             nc.vector.quantize_mx(out=w_codes[m][:].bitcast(FP8X4), scales=w_planes[m][:], in_=wg[m][:])
 
-        def fp8_pass(m):
-            for t0 in ((0,) if m < 2 else (0, H)):
-                bank, n = acc[m, t0]
-                nc.tensor.matmul_mx(
-                    out=bank[:],
-                    lhsT=w_codes[m][:].bitcast(FP8X4),
-                    lhsT_scale=w_planes[m][:],
-                    rhs=x_codes[:, t0 : t0 + n].bitcast(FP8X4),
-                    rhs_scale=x_planes[:, t0 : t0 + n],
-                    start=False,
-                    stop=True,
-                )
+        def fp8_pass(m, h, stop=True):
+            nc.tensor.matmul_mx(
+                out=acc[m, h][:],
+                lhsT=w_codes[m][:].bitcast(FP8X4),
+                lhsT_scale=w_planes[m][:],
+                rhs=x_codes[h][:].bitcast(FP8X4),
+                rhs_scale=x_planes[h][:],
+                start=False,
+                stop=stop,
+            )
 
-        def store(m):
-            nc.sync.dma_start(out=out[128 * m : 128 * m + 128, :], in_=res[m][:])
+        def round_pair(first, second, src):
+            interleave(nc.vector.tensor_copy, first, 0, src, 0, 128)
+            interleave(nc.scalar.copy, second, 64, src, 192, 64)
+            interleave(nc.vector.tensor_copy, second, 0, src, 128, 64)
 
         for m in range(4):
-            fp4_passes(m, (0, 1))
-        for h in range(2):
-            cast_x(2 * h)
-            cast_x(2 * h + 1)
-            quant_x(2 * h)
-            quant_x(2 * h + 1)
-        interleave(nc.vector.tensor_copy, wg[0], 0, w_raw[0], 0, 128)
-        interleave(nc.scalar.copy, wg[1], 32, w_raw[0], 160, 96)
-        interleave(nc.vector.tensor_copy, wg[1], 0, w_raw[0], 128, 32)
+            for h in range(2):
+                for a in (0, 1):
+                    fp4_pass(m, h, a)
+        round_pair(xg[0], xg[1], x_raw[0])
+        quant_x(0)
+        quant_x(1)
+        round_pair(wg[0], wg[1], w_raw[0])
         quant_w(0)
         quant_w(1)
+        round_pair(xg[2], xg[3], x_raw[1])
+        quant_x(2)
+        quant_x(3)
         for m in (2, 3):
             interleave(nc.vector.tensor_copy, wg[m], 0, w_raw[m - 1], 0, 128)
             quant_w(m)
-        for m in range(4):
-            fp4_passes(m, (2,))
-            fp8_pass(m)
         for m in (0, 1):
-            nc.scalar.copy(res[m][:], acc[m, 0][0][:])
-            store(m)
+            fp8_pass(m, 0, stop=False)
+        for m in (0, 1):
+            fp4_pass(m, 0, 2, stop=True)
+        for m in (0, 1):
+            fp4_pass(m, 1, 2)
+            fp8_pass(m, 1)
         for m in (2, 3):
-            nc.scalar.copy(res[m][:, 0:H], acc[m, 0][0][:])
-            nc.vector.tensor_copy(res[m][:, H:T], acc[m, H][0][:])
-            store(m)
+            for h in range(2):
+                fp4_pass(m, h, 2)
+            for h in range(2):
+                fp8_pass(m, h)
+        for h in range(2):
+            for m in (0, 1):
+                nc.scalar.copy(res_top[h][:, m, :], acc[m, h][:])
+            nc.sync.dma_start(out=out[0:256, H * h : H * (h + 1)].rearrange("(m p) t -> p m t", p=P), in_=res_top[h][:])
+        for m in (2, 3):
+            nc.scalar.copy(res[m][:, 0:H], acc[m, 0][:])
+            nc.vector.tensor_copy(res[m][:, H:T], acc[m, 1][:])
+            nc.sync.dma_start(out=out[128 * m : 128 * m + 128, :], in_=res[m][:])

@@ -27,7 +27,7 @@ def tile_mix_atom_fm_none_kernel(tc, x8, w8, x4_words, x4_scales, w4_words, w4_s
 
         x4w = [keep.tile([P, n * 2 * T], U8, align_bytes=64, name="x4w%d" % n) for n in (2, 1)]
         w4w = keep.tile([P, 2 * 2 * M], U8, align_bytes=64, name="w4w")
-        w4w_last = [keep.tile([P, M], U8, align_bytes=64, name="w4w_last%d" % h) for h in range(2)]
+        w4w_last = [keep.tile([P, 256 * n], U8, align_bytes=64, name="w4w_last%d" % h) for h, n in enumerate((3, 1)) if n]
         x4s = keep.tile([P, PASSES4 * T], U8, align_bytes=64, name="x4s")
         w4s = keep.tile([P, PASSES4 * M], U8, align_bytes=64, name="w4s")
         x_raw = [keep.tile([P, 4, H], F32, align_bytes=64, name="x_raw%d" % h) for h in range(2)]
@@ -58,10 +58,10 @@ def tile_mix_atom_fm_none_kernel(tc, x8, w8, x4_words, x4_scales, w4_words, w4_s
         nc.sync.dma_start(out=w_raw[0][:], in_=w8_rows[:, :, 0:256])
         nc.sync.dma_start(out=x_raw[1][:], in_=x8_rows[:, :, H:T])
         words(nc.sync, x4w[1], x4_words, 2, 3)
-        nc.sync.dma_start(out=w4w_last[0][:].bitcast(I32), in_=w4_words.bitcast(I32)[2, :, 0:128])
+        nc.sync.dma_start(out=w4w_last[0][:].bitcast(I32), in_=w4_words.bitcast(I32)[2, :, 0:192])
         nc.sync.dma_start(out=w_raw[1][:], in_=w8_rows[:, :, 256:384])
         nc.sync.dma_start(out=w_raw[2][:], in_=w8_rows[:, :, 384:512])
-        nc.sync.dma_start(out=w4w_last[1][:].bitcast(I32), in_=w4_words.bitcast(I32)[2, :, 128:256])
+        nc.sync.dma_start(out=w4w_last[1][:].bitcast(I32), in_=w4_words.bitcast(I32)[2, :, 192:256])
 
         acc = {}
         for m in range(4):
@@ -91,7 +91,7 @@ def tile_mix_atom_fm_none_kernel(tc, x8, w8, x4_words, x4_scales, w4_words, w4_s
             if a < 2:
                 w_words = w4w[:, c0 + 256 * m : c0 + 256 * m + 256]
             else:
-                w_words = w4w_last[m // 2][:, 256 * (m % 2) : 256 * (m % 2) + 256]
+                w_words = w4w_last[m // 3][:, 256 * (m % 3) : 256 * (m % 3) + 256]
             nc.tensor.matmul_mx(
                 out=acc[m, h][:],
                 lhsT=w_words.bitcast(FP4X4),
@@ -153,25 +153,28 @@ def tile_mix_atom_fm_none_kernel(tc, x8, w8, x4_words, x4_scales, w4_words, w4_s
         round_pair(xg[2], xg[3], x_raw[1])
         quant_x(2)
         quant_x(3)
-        for m in (2, 3):
-            interleave(nc.vector.tensor_copy, wg[m], 0, w_raw[m - 1], 0, 128)
-            quant_w(m)
         for m in (0, 1):
             fp8_pass(m, 0, stop=False)
         for m in (0, 1):
             fp4_pass(m, 0, 2, stop=True)
         for m in (0, 1):
             fp4_pass(m, 1, 2)
+        for m in (0, 1):
             fp8_pass(m, 1)
+        nc.vector.tensor_copy(res_top[0][:, 0, :], acc[0, 0][:])
+        nc.scalar.copy(res_top[0][:, 1, :], acc[1, 0][:])
+        nc.sync.dma_start(out=out[0:256, H * 0 : H * (0 + 1)].rearrange("(m p) t -> p m t", p=P), in_=res_top[0][:])
+        for m in (0, 1):
+            nc.scalar.copy(res_top[1][:, m, :], acc[m, 1][:])
+        nc.sync.dma_start(out=out[0:256, H * 1 : H * (1 + 1)].rearrange("(m p) t -> p m t", p=P), in_=res_top[1][:])
+        for m in (2, 3):
+            interleave(nc.vector.tensor_copy, wg[m], 0, w_raw[m - 1], 0, 128)
+            quant_w(m)
         for m in (2, 3):
             for h in range(2):
                 fp4_pass(m, h, 2)
             for h in range(2):
                 fp8_pass(m, h)
-        for h in range(2):
-            for m in (0, 1):
-                nc.scalar.copy(res_top[h][:, m, :], acc[m, h][:])
-            nc.sync.dma_start(out=out[0:256, H * h : H * (h + 1)].rearrange("(m p) t -> p m t", p=P), in_=res_top[h][:])
         for m in (2, 3):
             nc.scalar.copy(res[m][:, 0:H], acc[m, 0][:])
             nc.vector.tensor_copy(res[m][:, H:T], acc[m, 1][:])

@@ -161,15 +161,15 @@ def tile_mix_atom_fm_none_kernel(tc, x8, w8, x4_words, x4_scales, w4_words, w4_s
             fp4_pass(m, 1, 2)
         for m in (0, 1):
             fp8_pass(m, 1)
-        nc.vector.tensor_copy(res_top[0][:, 0, :], acc[0, 0][:])
-        nc.scalar.copy(res_top[0][:, 1, :], acc[1, 0][:])
-        nc.sync.dma_start(out=out[0:256, H * 0 : H * (0 + 1)].rearrange("(m p) t -> p m t", p=P), in_=res_top[0][:])
-        for m in (0, 1):
-            nc.scalar.copy(res_top[1][:, m, :], acc[m, 1][:])
-        nc.sync.dma_start(out=out[0:256, H * 1 : H * (1 + 1)].rearrange("(m p) t -> p m t", p=P), in_=res_top[1][:])
+        for h in range(2):
+            for m in (0, 1):
+                nc.scalar.copy(res_top[h][:, m, :], acc[m, h][:])
+            nc.sync.dma_start(out=out[0:256, H * h : H * (h + 1)].rearrange("(m p) t -> p m t", p=P), in_=res_top[h][:])
         for m in (2, 3):
-            interleave(nc.vector.tensor_copy, wg[m], 0, w_raw[m - 1], 0, 128)
-            quant_w(m)
+            for c in (0, 64):
+                interleave(nc.vector.tensor_copy, wg[m], c, w_raw[m - 1], c, 64)
+            for c in (0, 64):
+                nc.vector.quantize_mx(out=w_codes[m][:, c : c + 64].bitcast(FP8X4), scales=w_planes[m][:, c : c + 64], in_=wg[m][:, 4 * c : 4 * c + 256])
         for m in (2, 3):
             for h in range(2):
                 fp4_pass(m, h, 2)

@@ -66,22 +66,20 @@ def tile_mix_atom_fm_none_kernel(tc, x8, w8, x4_words, x4_scales, w4_words, w4_s
         acc = {}
         for m in range(4):
             for h in range(2):
-                acc[m, h] = psum.tile([P, H], F32, name="acc%d_%d" % (m, h))
+                acc[m, h] = psum.tile([P, T], F32, name="acc%d_%d" % (m, h))[:, 0:H] if (m, h) != (3, 1) else None
+        last_bank = psum.tile([P, T], F32, name="last_bank")
+        acc[3, 1] = last_bank[:, 0:H]
 
-        warm_in = keep.tile([P, 1024], BF16, align_bytes=64, name="warm_in")
-        warm_codes = keep.tile([P, 256], U32, align_bytes=64, name="warm_codes")
-        warm_planes = keep.tile([P, 256], U8, align_bytes=64, name="warm_planes")
-        nc.vector.memset(warm_in[:].bitcast(I32), 0)
         warm = keep.tile([P, 8], F32, name="warm")
-        nc.scalar.copy(warm[:, 0:1], warm_in[:, 0:2].bitcast(F32))
-        nc.vector.quantize_mx(out=warm_codes[:].bitcast(FP8X4), scales=warm_planes[:], in_=warm_in[:])
-        for i in range(16):
+        nc.vector.memset(warm[:, 0:1], 0.0)
+        nc.scalar.copy(warm[:, 1:2], warm[:, 0:1])
+        for i in range(3):
             nc.tensor.matmul_mx(
-                out=acc[3, 1][:],
-                lhsT=warm_codes[:, 0:128].bitcast(FP8X4),
-                lhsT_scale=warm_planes[:, 0:128],
-                rhs=warm_codes[:].bitcast(FP8X4),
-                rhs_scale=warm_planes[:],
+                out=last_bank[:],
+                lhsT=x4w[0][:, 0:256].bitcast(FP4X4),
+                lhsT_scale=x4s[:, 0:128],
+                rhs=x4w[0][:, 0:1024].bitcast(FP4X4),
+                rhs_scale=x4s[:, 0:512],
                 start=True,
                 stop=True,
             )
@@ -93,7 +91,7 @@ def tile_mix_atom_fm_none_kernel(tc, x8, w8, x4_words, x4_scales, w4_words, w4_s
             else:
                 w_words = w4w_last[m // 3][:, 256 * (m % 3) : 256 * (m % 3) + 256]
             nc.tensor.matmul_mx(
-                out=acc[m, h][:],
+                out=acc[m, h],
                 lhsT=w_words.bitcast(FP4X4),
                 lhsT_scale=w4s[:, 512 * a + 128 * m : 512 * a + 128 * m + 128],
                 rhs=x4w[a // 2][:, c0 + 2 * H * h : c0 + 2 * H * (h + 1)].bitcast(FP4X4),
@@ -126,7 +124,7 @@ def tile_mix_atom_fm_none_kernel(tc, x8, w8, x4_words, x4_scales, w4_words, w4_s
 
         def fp8_pass(m, h, stop=True):
             nc.tensor.matmul_mx(
-                out=acc[m, h][:],
+                out=acc[m, h],
                 lhsT=w_codes[m][:].bitcast(FP8X4),
                 lhsT_scale=w_planes[m][:],
                 rhs=x_codes[h][:].bitcast(FP8X4),
@@ -140,10 +138,9 @@ def tile_mix_atom_fm_none_kernel(tc, x8, w8, x4_words, x4_scales, w4_words, w4_s
             interleave(nc.scalar.copy, second, 64, src, 192, 64)
             interleave(nc.vector.tensor_copy, second, 0, src, 128, 64)
 
-        for m in range(4):
-            for h in range(2):
-                for a in (0, 1):
-                    fp4_pass(m, h, a)
+        for m, h in ((0, 0), (1, 0), (0, 1), (1, 1), (2, 0), (2, 1), (3, 0)):
+            for a in (0, 1):
+                fp4_pass(m, h, a)
         round_pair(xg[0], xg[1], x_raw[0])
         quant_x(0)
         quant_x(1)
@@ -161,9 +158,11 @@ def tile_mix_atom_fm_none_kernel(tc, x8, w8, x4_words, x4_scales, w4_words, w4_s
             fp4_pass(m, 1, 2)
         for m in (0, 1):
             fp8_pass(m, 1)
+        for a in (0, 1):
+            fp4_pass(3, 1, a)
         for h in range(2):
             for m in (0, 1):
-                nc.scalar.copy(res_top[h][:, m, :], acc[m, h][:])
+                nc.scalar.copy(res_top[h][:, m, :], acc[m, h])
             nc.sync.dma_start(out=out[0:256, H * h : H * (h + 1)].rearrange("(m p) t -> p m t", p=P), in_=res_top[h][:])
         for m in (2, 3):
             for c in (0, 64):
@@ -176,6 +175,6 @@ def tile_mix_atom_fm_none_kernel(tc, x8, w8, x4_words, x4_scales, w4_words, w4_s
             for h in range(2):
                 fp8_pass(m, h)
         for m in (2, 3):
-            nc.scalar.copy(res[m][:, 0:H], acc[m, 0][:])
-            nc.vector.tensor_copy(res[m][:, H:T], acc[m, 1][:])
+            nc.scalar.copy(res[m][:, 0:H], acc[m, 0])
+            nc.vector.tensor_copy(res[m][:, H:T], acc[m, 1])
             nc.sync.dma_start(out=out[128 * m : 128 * m + 128, :], in_=res[m][:])

@@ -44,15 +44,15 @@ def tile_mix_atom_fm_none_kernel(tc, x8, w8, x4_words, x4_scales, w4_words, w4_s
         def scale_rows(queue, plane, rows, r):
             queue.dma_start(out=plane[r:P:32, :].bitcast(I32).rearrange("p (a n) -> p a n", a=PASSES4), in_=rows[r])
 
-        words(nc.gpsimd, w4w, w4_words, 0, 2)
         scale_rows(nc.scalar, x4s, x4s_rows, 0)
         scale_rows(nc.sync, x4s, x4s_rows, 1)
         scale_rows(nc.scalar, x4s, x4s_rows, 2)
-        words(nc.sync, x4w[0], x4_words, 0, 2)
         scale_rows(nc.sync, x4s, x4s_rows, 3)
+        words(nc.sync, x4w[0], x4_words, 0, 2)
         scale_rows(nc.sync, w4s, w4s_rows, 0)
-        scale_rows(nc.sync, w4s, w4s_rows, 1)
+        words(nc.sync, w4w, w4_words, 0, 2)
         nc.sync.dma_start(out=x_raw[0][:], in_=x8_rows[:, :, 0:H])
+        scale_rows(nc.sync, w4s, w4s_rows, 1)
         scale_rows(nc.sync, w4s, w4s_rows, 2)
         scale_rows(nc.sync, w4s, w4s_rows, 3)
         nc.sync.dma_start(out=w_raw[0][:], in_=w8_rows[:, :, 0:256])
@@ -70,9 +70,6 @@ def tile_mix_atom_fm_none_kernel(tc, x8, w8, x4_words, x4_scales, w4_words, w4_s
         last_bank = psum.tile([P, T], F32, name="last_bank")
         acc[3, 1] = last_bank[:, 0:H]
 
-        warm = keep.tile([P, 8], F32, name="warm")
-        nc.vector.memset(warm[:, 0:1], 0.0)
-        nc.scalar.copy(warm[:, 1:2], warm[:, 0:1])
         for i in range(3):
             nc.tensor.matmul_mx(
                 out=last_bank[:],

@@ -47,7 +47,7 @@ def tile_mix_atom_fm_none_kernel(tc, x8, w8, x4_words, x4_scales, w4_words, w4_s
         scale_rows(nc.scalar, x4s, x4s_rows, 0)
         scale_rows(nc.sync, x4s, x4s_rows, 1)
         scale_rows(nc.scalar, x4s, x4s_rows, 2)
-        scale_rows(nc.sync, x4s, x4s_rows, 3)
+        scale_rows(nc.scalar, x4s, x4s_rows, 3)
         words(nc.sync, x4w[0], x4_words, 0, 2)
         scale_rows(nc.sync, w4s, w4s_rows, 0)
         words(nc.sync, w4w, w4_words, 0, 2)

@@ -25,13 +25,13 @@ def tile_mix_atom_fm_none_kernel(tc, x8, w8, x4_words, x4_scales, w4_words, w4_s
         psum = ctx.enter_context(tc.psum_pool(name="psum", bufs=1))
         ctx.enter_context(tc.manual_schedule())
 
-        x4w = [keep.tile([P, n * 2 * T], U8, align_bytes=64, name="x4w%d" % n) for n in (2, 1)]
-        w4w = keep.tile([P, 2 * 2 * M], U8, align_bytes=64, name="w4w")
-        w4w_last = [keep.tile([P, 256 * n], U8, align_bytes=64, name="w4w_last%d" % h) for h, n in enumerate((3, 1)) if n]
-        x4s = keep.tile([P, PASSES4 * T], U8, align_bytes=64, name="x4s")
-        w4s = keep.tile([P, PASSES4 * M], U8, align_bytes=64, name="w4s")
-        x_raw = [keep.tile([P, 4, H], F32, align_bytes=64, name="x_raw%d" % h) for h in range(2)]
-        w_raw = [keep.tile([P, 4, n], F32, align_bytes=64, name="w_raw%d" % h) for h, n in enumerate((256, 128, 128))]
+        x4w = [keep.tile([P, n * 2 * T], U8, align_bytes=256, name="x4w%d" % n) for n in (2, 1)]
+        w4w = keep.tile([P, 2 * 2 * M], U8, align_bytes=256, name="w4w")
+        w4w_last = [keep.tile([P, 256 * n], U8, align_bytes=256, name="w4w_last%d" % h) for h, n in enumerate((3, 1)) if n]
+        x4s = keep.tile([P, PASSES4 * T], U8, align_bytes=256, name="x4s")
+        w4s = keep.tile([P, PASSES4 * M], U8, align_bytes=256, name="w4s")
+        x_raw = [keep.tile([P, 4, H], F32, align_bytes=256, name="x_raw%d" % h) for h in range(2)]
+        w_raw = [keep.tile([P, 4, n], F32, align_bytes=256, name="w_raw%d" % h) for h, n in enumerate((256, 128, 128))]
 
         x8_rows = x8.rearrange("(p j) t -> p j t", j=4)
         w8_rows = w8.rearrange("(p j) n -> p j n", j=4)
@@ -103,14 +103,14 @@ def tile_mix_atom_fm_none_kernel(tc, x8, w8, x4_words, x4_scales, w4_words, w4_s
                 src[:, :, s0 : s0 + n].rearrange("p t (c i) -> p c t i", i=4),
             )
 
-        x_codes = [keep.tile([P, H], U32, align_bytes=64, name="x_codes%d" % h) for h in range(2)]
-        x_planes = [keep.tile([P, H], U8, align_bytes=64, name="x_planes%d" % h) for h in range(2)]
-        xg = [keep.tile([P, 512], BF16, align_bytes=64, name="xg%d" % h) for h in range(4)]
-        w_codes = [keep.tile([P, 128], U32, align_bytes=64, name="w_codes%d" % m) for m in range(4)]
-        w_planes = [keep.tile([P, 128], U8, align_bytes=64, name="w_planes%d" % m) for m in range(4)]
-        wg = [keep.tile([P, 512], BF16, align_bytes=64, name="wg%d" % m) for m in range(4)]
-        res_top = [keep.tile([P, 2, H], F32, name="res_top%d" % h) for h in range(2)]
-        res = {m: keep.tile([P, T], F32, name="res%d" % m) for m in (2, 3)}
+        x_codes = [keep.tile([P, H], U32, align_bytes=256, name="x_codes%d" % h) for h in range(2)]
+        x_planes = [keep.tile([P, H], U8, align_bytes=256, name="x_planes%d" % h) for h in range(2)]
+        xg = [keep.tile([P, 512], BF16, align_bytes=256, name="xg%d" % h) for h in range(4)]
+        w_codes = [keep.tile([P, 128], U32, align_bytes=256, name="w_codes%d" % m) for m in range(4)]
+        w_planes = [keep.tile([P, 128], U8, align_bytes=256, name="w_planes%d" % m) for m in range(4)]
+        wg = [keep.tile([P, 512], BF16, align_bytes=256, name="wg%d" % m) for m in range(4)]
+        res_top = [keep.tile([P, 2, H], F32, align_bytes=256, name="res_top%d" % h) for h in range(2)]
+        res = {m: keep.tile([P, T], F32, align_bytes=256, name="res%d" % m) for m in (2, 3)}
 
         def quant_x(q):
             cols = slice(128 * (q % 2), 128 * (q % 2) + 128)

@@ -135,9 +135,11 @@ def tile_mix_atom_fm_none_kernel(tc, x8, w8, x4_words, x4_scales, w4_words, w4_s
             interleave(nc.scalar.copy, second, 64, src, 192, 64)
             interleave(nc.vector.tensor_copy, second, 0, src, 128, 64)
 
-        for m, h in ((0, 0), (1, 0), (0, 1), (1, 1), (2, 0), (2, 1), (3, 0)):
+        for m, h in ((0, 0), (1, 0), (0, 1), (1, 1), (2, 0), (2, 1)):
             for a in (0, 1):
                 fp4_pass(m, h, a)
+        for h in range(2):
+            fp4_pass(3, h, 0)
         round_pair(xg[0], xg[1], x_raw[0])
         quant_x(0)
         quant_x(1)
@@ -155,8 +157,6 @@ def tile_mix_atom_fm_none_kernel(tc, x8, w8, x4_words, x4_scales, w4_words, w4_s
             fp4_pass(m, 1, 2)
         for m in (0, 1):
             fp8_pass(m, 1)
-        for a in (0, 1):
-            fp4_pass(3, 1, a)
         for h in range(2):
             for m in (0, 1):
                 nc.scalar.copy(res_top[h][:, m, :], acc[m, h])
@@ -166,12 +166,16 @@ def tile_mix_atom_fm_none_kernel(tc, x8, w8, x4_words, x4_scales, w4_words, w4_s
                 interleave(nc.vector.tensor_copy, wg[m], c, w_raw[m - 1], c, 64)
             for c in (0, 64):
                 nc.vector.quantize_mx(out=w_codes[m][:, c : c + 64].bitcast(FP8X4), scales=w_planes[m][:, c : c + 64], in_=wg[m][:, 4 * c : 4 * c + 256])
-        for m in (2, 3):
-            for h in range(2):
-                fp4_pass(m, h, 2)
+        for m, late in ((2, (2,)), (3, (1, 2))):
+            for a in late:
+                for h in range(2):
+                    fp4_pass(m, h, a)
             for h in range(2):
                 fp8_pass(m, h)
-        for m in (2, 3):
-            nc.scalar.copy(res[m][:, 0:H], acc[m, 0])
-            nc.vector.tensor_copy(res[m][:, H:T], acc[m, 1])
-            nc.sync.dma_start(out=out[128 * m : 128 * m + 128, :], in_=res[m][:])
+        nc.scalar.copy(res[2][:, 0:H], acc[2, 0])
+        nc.vector.tensor_copy(res[2][:, H:T], acc[2, 1])
+        nc.sync.dma_start(out=out[256:384, :], in_=res[2][:])
+        nc.vector.tensor_copy(res[3][:, 0:H], acc[3, 0])
+        nc.sync.dma_start(out=out[384:512, 0:H], in_=res[3][:, 0:H])
+        nc.scalar.copy(res[3][:, H:T], acc[3, 1])
+        nc.scalar.dma_start(out=out[384:512, H:T], in_=res[3][:, H:T])

@@ -25,13 +25,13 @@ def tile_mix_atom_fm_none_kernel(tc, x8, w8, x4_words, x4_scales, w4_words, w4_s
         psum = ctx.enter_context(tc.psum_pool(name="psum", bufs=1))
         ctx.enter_context(tc.manual_schedule())
 
-        x4w = [keep.tile([P, n * 2 * T], U8, align_bytes=256, name="x4w%d" % n) for n in (2, 1)]
-        w4w = keep.tile([P, 2 * 2 * M], U8, align_bytes=256, name="w4w")
-        w4w_last = [keep.tile([P, 256 * n], U8, align_bytes=256, name="w4w_last%d" % h) for h, n in enumerate((3, 1)) if n]
-        x4s = keep.tile([P, PASSES4 * T], U8, align_bytes=256, name="x4s")
-        w4s = keep.tile([P, PASSES4 * M], U8, align_bytes=256, name="w4s")
-        x_raw = [keep.tile([P, 4, H], F32, align_bytes=256, name="x_raw%d" % h) for h in range(2)]
-        w_raw = [keep.tile([P, 4, n], F32, align_bytes=256, name="w_raw%d" % h) for h, n in enumerate((256, 128, 128))]
+        x4w = [keep.tile([P, n * 2 * T], U8, align_bytes=1024, name="x4w%d" % n) for n in (2, 1)]
+        w4w = keep.tile([P, 2 * 2 * M], U8, align_bytes=1024, name="w4w")
+        w4w_last = [keep.tile([P, 256 * n], U8, align_bytes=1024, name="w4w_last%d" % h) for h, n in enumerate((3, 1)) if n]
+        x4s = keep.tile([P, PASSES4 * T], U8, align_bytes=1024, name="x4s")
+        w4s = keep.tile([P, PASSES4 * M], U8, align_bytes=1024, name="w4s")
+        x_raw = [keep.tile([P, 4, H], F32, align_bytes=1024, name="x_raw%d" % h) for h in range(2)]
+        w_raw = [keep.tile([P, 4, n], F32, align_bytes=1024, name="w_raw%d" % h) for h, n in enumerate((256, 128, 128))]
 
         x8_rows = x8.rearrange("(p j) t -> p j t", j=4)
         w8_rows = w8.rearrange("(p j) n -> p j n", j=4)
@@ -103,14 +103,14 @@ def tile_mix_atom_fm_none_kernel(tc, x8, w8, x4_words, x4_scales, w4_words, w4_s
                 src[:, :, s0 : s0 + n].rearrange("p t (c i) -> p c t i", i=4),
             )
 
-        x_codes = [keep.tile([P, H], U32, align_bytes=256, name="x_codes%d" % h) for h in range(2)]
-        x_planes = [keep.tile([P, H], U8, align_bytes=256, name="x_planes%d" % h) for h in range(2)]
-        xg = [keep.tile([P, 512], BF16, align_bytes=256, name="xg%d" % h) for h in range(4)]
-        w_codes = [keep.tile([P, 128], U32, align_bytes=256, name="w_codes%d" % m) for m in range(4)]
-        w_planes = [keep.tile([P, 128], U8, align_bytes=256, name="w_planes%d" % m) for m in range(4)]
-        wg = [keep.tile([P, 512], BF16, align_bytes=256, name="wg%d" % m) for m in range(4)]
-        res_top = [keep.tile([P, 2, H], F32, align_bytes=256, name="res_top%d" % h) for h in range(2)]
-        res = {m: keep.tile([P, T], F32, align_bytes=256, name="res%d" % m) for m in (2, 3)}
+        x_codes = [keep.tile([P, H], U32, align_bytes=1024, name="x_codes%d" % h) for h in range(2)]
+        x_planes = [keep.tile([P, H], U8, align_bytes=1024, name="x_planes%d" % h) for h in range(2)]
+        xg = [keep.tile([P, 512], BF16, align_bytes=1024, name="xg%d" % h) for h in range(4)]
+        w_codes = [keep.tile([P, 128], U32, align_bytes=1024, name="w_codes%d" % m) for m in range(4)]
+        w_planes = [keep.tile([P, 128], U8, align_bytes=1024, name="w_planes%d" % m) for m in range(4)]
+        wg = [keep.tile([P, 512], BF16, align_bytes=1024, name="wg%d" % m) for m in range(4)]
+        res_top = [keep.tile([P, 2, H], F32, align_bytes=1024, name="res_top%d" % h) for h in range(2)]
+        res = {m: keep.tile([P, T], F32, align_bytes=1024, name="res%d" % m) for m in (2, 3)}
 
         def quant_x(q):
             cols = slice(128 * (q % 2), 128 * (q % 2) + 128)

@@ -172,9 +172,9 @@ def tile_mix_atom_fm_none_kernel(tc, x8, w8, x4_words, x4_scales, w4_words, w4_s
                     fp4_pass(m, h, a)
             for h in range(2):
                 fp8_pass(m, h)
-        nc.scalar.copy(res[2][:, 0:H], acc[2, 0])
-        nc.vector.tensor_copy(res[2][:, H:T], acc[2, 1])
-        nc.sync.dma_start(out=out[256:384, :], in_=res[2][:])
+        for h in range(2):
+            nc.scalar.copy(res[2][:, H * h : H * (h + 1)], acc[2, h])
+            nc.sync.dma_start(out=out[256:384, H * h : H * (h + 1)], in_=res[2][:, H * h : H * (h + 1)])
         nc.vector.tensor_copy(res[3][:, 0:H], acc[3, 0])
         nc.sync.dma_start(out=out[384:512, 0:H], in_=res[3][:, 0:H])
         nc.scalar.copy(res[3][:, H:T], acc[3, 1])

@@ -174,7 +174,7 @@ def tile_mix_atom_fm_none_kernel(tc, x8, w8, x4_words, x4_scales, w4_words, w4_s
                 fp8_pass(m, h)
         for h in range(2):
             nc.scalar.copy(res[2][:, H * h : H * (h + 1)], acc[2, h])
-            nc.sync.dma_start(out=out[256:384, H * h : H * (h + 1)], in_=res[2][:, H * h : H * (h + 1)])
+        nc.sync.dma_start(out=out[256:384, :], in_=res[2][:])
         nc.vector.tensor_copy(res[3][:, 0:H], acc[3, 0])
         nc.sync.dma_start(out=out[384:512, 0:H], in_=res[3][:, 0:H])
         nc.scalar.copy(res[3][:, H:T], acc[3, 1])

@@ -70,13 +70,17 @@ def tile_mix_atom_fm_none_kernel(tc, x8, w8, x4_words, x4_scales, w4_words, w4_s
         last_bank = psum.tile([P, T], F32, name="last_bank")
         acc[3, 1] = last_bank[:, 0:H]
 
+        zeros = keep.tile([P, T + 64], U32, align_bytes=1024, name="zeros")
+        zeros_plane = keep.tile([P, 32], U8, align_bytes=1024, name="zeros_plane")
+        nc.vector.memset(zeros[:], 0)
+        nc.vector.quantize_mx(out=zeros[:, 0:32].bitcast(FP8X4), scales=zeros_plane[:], in_=zeros[:, T : T + 64].bitcast(BF16))
         for i in range(3):
             nc.tensor.matmul_mx(
-                out=last_bank[:],
-                lhsT=x4w[0][:, 0:256].bitcast(FP4X4),
-                lhsT_scale=x4s[:, 0:128],
-                rhs=x4w[0][:, 0:1024].bitcast(FP4X4),
-                rhs_scale=x4s[:, 0:512],
+                out=last_bank[0:32, :],
+                lhsT=zeros[:, 0:32].bitcast(FP8X4),
+                lhsT_scale=zeros_plane[:],
+                rhs=zeros[:, 0:T].bitcast(FP8X4),
+                rhs_scale=x4s[:, 0:T],
                 start=True,
                 stop=True,
             )

@@ -70,17 +70,17 @@ def tile_mix_atom_fm_none_kernel(tc, x8, w8, x4_words, x4_scales, w4_words, w4_s
         last_bank = psum.tile([P, T], F32, name="last_bank")
         acc[3, 1] = last_bank[:, 0:H]
 
-        zeros = keep.tile([P, T + 64], U32, align_bytes=1024, name="zeros")
-        zeros_plane = keep.tile([P, 32], U8, align_bytes=1024, name="zeros_plane")
+        zeros = keep.tile([P, T + 64 + T // 4], U32, align_bytes=1024, name="zeros")
+        zeros_plane = zeros[:, T + 64 :].bitcast(U8)
         nc.vector.memset(zeros[:], 0)
-        nc.vector.quantize_mx(out=zeros[:, 0:32].bitcast(FP8X4), scales=zeros_plane[:], in_=zeros[:, T : T + 64].bitcast(BF16))
-        for i in range(3):
+        nc.vector.quantize_mx(out=zeros[:, 0:32].bitcast(FP8X4), scales=zeros_plane[:, 0:32], in_=zeros[:, T : T + 64].bitcast(BF16))
+        for i in range(6):
             nc.tensor.matmul_mx(
                 out=last_bank[0:32, :],
                 lhsT=zeros[:, 0:32].bitcast(FP8X4),
-                lhsT_scale=zeros_plane[:],
+                lhsT_scale=zeros_plane[:, 0:32],
                 rhs=zeros[:, 0:T].bitcast(FP8X4),
-                rhs_scale=x4s[:, 0:T],
+                rhs_scale=zeros_plane,
                 start=True,
                 stop=True,
             )
@@ -144,6 +144,7 @@ def tile_mix_atom_fm_none_kernel(tc, x8, w8, x4_words, x4_scales, w4_words, w4_s
                 fp4_pass(m, h, a)
         for h in range(2):
             fp4_pass(3, h, 0)
+            fp4_pass(3, h, 1)
         round_pair(xg[0], xg[1], x_raw[0])
         quant_x(0)
         quant_x(1)
@@ -170,14 +171,14 @@ def tile_mix_atom_fm_none_kernel(tc, x8, w8, x4_words, x4_scales, w4_words, w4_s
                 interleave(nc.vector.tensor_copy, wg[m], c, w_raw[m - 1], c, 64)
             for c in (0, 64):
                 nc.vector.quantize_mx(out=w_codes[m][:, c : c + 64].bitcast(FP8X4), scales=w_planes[m][:, c : c + 64], in_=wg[m][:, 4 * c : 4 * c + 256])
-        for m, late in ((2, (2,)), (3, (1, 2))):
+        for m, late in ((2, (2,)), (3, (2,))):
             for a in late:
                 for h in range(2):
                     fp4_pass(m, h, a)
             for h in range(2):
                 fp8_pass(m, h)
-        for h in range(2):
-            nc.scalar.copy(res[2][:, H * h : H * (h + 1)], acc[2, h])
+        nc.scalar.copy(res[2][:, 0:H], acc[2, 0])
+        nc.vector.tensor_copy(res[2][:, H:T], acc[2, 1])
         nc.sync.dma_start(out=out[256:384, :], in_=res[2][:])
         nc.vector.tensor_copy(res[3][:, 0:H], acc[3, 0])
         nc.sync.dma_start(out=out[384:512, 0:H], in_=res[3][:, 0:H])

from contextlib import ExitStack

import concourse.mybir as mybir

O, K4, M, T = 512, 1536, 512, 512
FLOPS = 2 * M * T * (O + K4)

F32 = mybir.dt.float32
BF16 = mybir.dt.bfloat16
U32 = mybir.dt.uint32
I32 = mybir.dt.int32
U8 = mybir.dt.uint8
FP8X4 = mybir.dt.float8_e4m3fn_x4
FP4X4 = mybir.dt.float4_e2m1fn_x4

P = 128
PASSES4 = K4 // 512
H = T // 2


def tile_mix_atom_fm_none_kernel(tc, x8, w8, x4_words, x4_scales, w4_words, w4_scales, out):
    nc = tc.nc
    with ExitStack() as ctx:
        keep = ctx.enter_context(tc.tile_pool(name="keep", bufs=1))
        psum = ctx.enter_context(tc.psum_pool(name="psum", bufs=1))
        ctx.enter_context(tc.manual_schedule())

        x4w = [keep.tile([P, n * 2 * T], U8, align_bytes=1024, name="x4w%d" % n) for n in (2, 1)]
        w4w = keep.tile([P, 2 * 2 * M], U8, align_bytes=1024, name="w4w")
        w4w_last = [keep.tile([P, 256 * n], U8, align_bytes=1024, name="w4w_last%d" % h) for h, n in enumerate((3, 1)) if n]
        x4s = keep.tile([P, PASSES4 * T], U8, align_bytes=1024, name="x4s")
        w4s = keep.tile([P, PASSES4 * M], U8, align_bytes=1024, name="w4s")
        x_raw = [keep.tile([P, 4, H], F32, align_bytes=1024, name="x_raw%d" % h) for h in range(2)]
        w_raw = [keep.tile([P, 4, n], F32, align_bytes=1024, name="w_raw%d" % h) for h, n in enumerate((256, 128, 128))]

        x8_rows = x8.rearrange("(p j) t -> p j t", j=4)
        w8_rows = w8.rearrange("(p j) n -> p j n", j=4)
        x4s_rows = x4_scales.bitcast(I32).rearrange("a (q r) n -> r q a n", r=4)
        w4s_rows = w4_scales.bitcast(I32).rearrange("a (q r) n -> r q a n", r=4)

        def words(queue, tile, src, a0, a1):
            queue.dma_start(out=tile[:].bitcast(I32).rearrange("p (a c) -> p a c", a=a1 - a0), in_=src.bitcast(I32)[a0:a1].rearrange("a p c -> p a c"))

        def scale_rows(queue, plane, rows, r):
            queue.dma_start(out=plane[r:P:32, :].bitcast(I32).rearrange("p (a n) -> p a n", a=PASSES4), in_=rows[r])

        scale_rows(nc.scalar, x4s, x4s_rows, 0)
        scale_rows(nc.sync, x4s, x4s_rows, 1)
        scale_rows(nc.scalar, x4s, x4s_rows, 2)
        scale_rows(nc.scalar, x4s, x4s_rows, 3)
        words(nc.sync, x4w[0], x4_words, 0, 2)
        scale_rows(nc.sync, w4s, w4s_rows, 0)
        words(nc.sync, w4w, w4_words, 0, 2)
        nc.sync.dma_start(out=x_raw[0][:], in_=x8_rows[:, :, 0:H])
        scale_rows(nc.sync, w4s, w4s_rows, 1)
        scale_rows(nc.sync, w4s, w4s_rows, 2)
        scale_rows(nc.sync, w4s, w4s_rows, 3)
        nc.sync.dma_start(out=w_raw[0][:], in_=w8_rows[:, :, 0:256])
        nc.sync.dma_start(out=x_raw[1][:], in_=x8_rows[:, :, H:T])
        words(nc.sync, x4w[1], x4_words, 2, 3)
        nc.sync.dma_start(out=w4w_last[0][:].bitcast(I32), in_=w4_words.bitcast(I32)[2, :, 0:192])
        nc.sync.dma_start(out=w_raw[1][:], in_=w8_rows[:, :, 256:384])
        nc.sync.dma_start(out=w_raw[2][:], in_=w8_rows[:, :, 384:512])
        nc.sync.dma_start(out=w4w_last[1][:].bitcast(I32), in_=w4_words.bitcast(I32)[2, :, 192:256])

        acc = {}
        for m in range(4):
            for h in range(2):
                acc[m, h] = psum.tile([P, T], F32, name="acc%d_%d" % (m, h))[:, 0:H] if (m, h) != (3, 1) else None
        last_bank = psum.tile([P, T], F32, name="last_bank")
        acc[3, 1] = last_bank[:, 0:H]

        zeros = keep.tile([P, T + 64 + T // 4], U32, align_bytes=1024, name="zeros")
        zeros_plane = zeros[:, T + 64 :].bitcast(U8)
        nc.vector.memset(zeros[:], 0)
        nc.vector.quantize_mx(out=zeros[:, 0:32].bitcast(FP8X4), scales=zeros_plane[:, 0:32], in_=zeros[:, T : T + 64].bitcast(BF16))
        for i in range(6):
            nc.tensor.matmul_mx(
                out=last_bank[0:32, :],
                lhsT=zeros[:, 0:32].bitcast(FP8X4),
                lhsT_scale=zeros_plane[:, 0:32],
                rhs=zeros[:, 0:T].bitcast(FP8X4),
                rhs_scale=zeros_plane,
                start=True,
                stop=True,
            )

        def fp4_pass(m, h, a, stop=False):
            c0 = 1024 * (a % 2)
            if a < 2:
                w_words = w4w[:, c0 + 256 * m : c0 + 256 * m + 256]
            else:
                w_words = w4w_last[m // 3][:, 256 * (m % 3) : 256 * (m % 3) + 256]
            nc.tensor.matmul_mx(
                out=acc[m, h],
                lhsT=w_words.bitcast(FP4X4),
                lhsT_scale=w4s[:, 512 * a + 128 * m : 512 * a + 128 * m + 128],
                rhs=x4w[a // 2][:, c0 + 2 * H * h : c0 + 2 * H * (h + 1)].bitcast(FP4X4),
                rhs_scale=x4s[:, 512 * a + H * h : 512 * a + H * (h + 1)],
                start=(a == 0),
                stop=stop,
            )

        def interleave(copy, dst, c0, src, s0, n):
            copy(
                dst[:, 4 * c0 : 4 * (c0 + n)].rearrange("p (c i t) -> p c t i", i=4, t=4),
                src[:, :, s0 : s0 + n].rearrange("p t (c i) -> p c t i", i=4),
            )

        x_codes = [keep.tile([P, H], U32, align_bytes=1024, name="x_codes%d" % h) for h in range(2)]
        x_planes = [keep.tile([P, H], U8, align_bytes=1024, name="x_planes%d" % h) for h in range(2)]
        xg = [keep.tile([P, 512], BF16, align_bytes=1024, name="xg%d" % h) for h in range(4)]
        w_codes = [keep.tile([P, 128], U32, align_bytes=1024, name="w_codes%d" % m) for m in range(4)]
        w_planes = [keep.tile([P, 128], U8, align_bytes=1024, name="w_planes%d" % m) for m in range(4)]
        wg = [keep.tile([P, 512], BF16, align_bytes=1024, name="wg%d" % m) for m in range(4)]
        res_top = [keep.tile([P, 2, H], F32, align_bytes=1024, name="res_top%d" % h) for h in range(2)]
        res = {m: keep.tile([P, T], F32, align_bytes=1024, name="res%d" % m) for m in (2, 3)}

        def quant_x(q):
            cols = slice(128 * (q % 2), 128 * (q % 2) + 128)
            nc.vector.quantize_mx(out=x_codes[q // 2][:, cols].bitcast(FP8X4), scales=x_planes[q // 2][:, cols], in_=xg[q][:])

        def quant_w(m):
            nc.vector.quantize_mx(out=w_codes[m][:].bitcast(FP8X4), scales=w_planes[m][:], in_=wg[m][:])

        def fp8_pass(m, h, stop=True):
            nc.tensor.matmul_mx(
                out=acc[m, h],
                lhsT=w_codes[m][:].bitcast(FP8X4),
                lhsT_scale=w_planes[m][:],
                rhs=x_codes[h][:].bitcast(FP8X4),
                rhs_scale=x_planes[h][:],
                start=False,
                stop=stop,
            )

        def round_pair(first, second, src):
            interleave(nc.vector.tensor_copy, first, 0, src, 0, 128)
            interleave(nc.scalar.copy, second, 64, src, 192, 64)
            interleave(nc.vector.tensor_copy, second, 0, src, 128, 64)

        for m, h in ((0, 0), (1, 0), (0, 1), (1, 1), (2, 0), (2, 1)):
            for a in (0, 1):
                fp4_pass(m, h, a)
        for h in range(2):
            fp4_pass(3, h, 0)
            fp4_pass(3, h, 1)
        round_pair(xg[0], xg[1], x_raw[0])
        quant_x(0)
        quant_x(1)
        round_pair(wg[0], wg[1], w_raw[0])
        quant_w(0)
        quant_w(1)
        round_pair(xg[2], xg[3], x_raw[1])
        quant_x(2)
        quant_x(3)
        for m in (0, 1):
            fp8_pass(m, 0, stop=False)
        for m in (0, 1):
            fp4_pass(m, 0, 2, stop=True)
        for m in (0, 1):
            fp4_pass(m, 1, 2)
        for m in (0, 1):
            fp8_pass(m, 1)
        for h in range(2):
            for m in (0, 1):
                nc.scalar.copy(res_top[h][:, m, :], acc[m, h])
            nc.sync.dma_start(out=out[0:256, H * h : H * (h + 1)].rearrange("(m p) t -> p m t", p=P), in_=res_top[h][:])
        for m in (2, 3):
            for c in (0, 64):
                interleave(nc.vector.tensor_copy, wg[m], c, w_raw[m - 1], c, 64)
            for c in (0, 64):
                nc.vector.quantize_mx(out=w_codes[m][:, c : c + 64].bitcast(FP8X4), scales=w_planes[m][:, c : c + 64], in_=wg[m][:, 4 * c : 4 * c + 256])
        for m, late in ((2, (2,)), (3, (2,))):
            for a in late:
                for h in range(2):
                    fp4_pass(m, h, a)
            for h in range(2):
                fp8_pass(m, h)
        nc.scalar.copy(res[2][:, 0:H], acc[2, 0])
        nc.vector.tensor_copy(res[2][:, H:T], acc[2, 1])
        nc.sync.dma_start(out=out[256:384, :], in_=res[2][:])
        nc.vector.tensor_copy(res[3][:, 0:H], acc[3, 0])
        nc.sync.dma_start(out=out[384:512, 0:H], in_=res[3][:, 0:H])
        nc.scalar.copy(res[3][:, H:T], acc[3, 1])
        nc.scalar.dma_start(out=out[384:512, H:T], in_=res[3][:, H:T])
